import numpy as np, ml_dtypes
CORES = [113,118,241,246]
N = 4
BF = ml_dtypes.bfloat16
def gentries(a):
    return np.ascontiguousarray(a.reshape(8, 16, -1).transpose(0, 2, 1)).reshape(8, -1)
def gtable(e):
    e = np.asarray(e); return np.ascontiguousarray(e.reshape(8, -1, 16).transpose(0, 2, 1)).reshape(128, -1).astype(np.int32)
V, RO, HOP = 1536, 2, 2
W = N * V
def rings(o, cut):
    t = np.arange(W); c = cut.copy(); c[0] = True
    first = np.maximum.accumulate(np.where(c, t, 0)); nt = np.where(np.append(c[1:], True), first, t + 1)
    nx = np.empty(W, np.int64); pv = np.empty(W, np.int64); nx[o] = o[nt]; pv[o[nt]] = o
    return nx, pv
def walk(rng, n, step):
    w = np.add.accumulate(rng.integers(-step, step + 1, (16, n)), axis=1) + rng.integers(0, 256, (16, 1))
    return np.abs((w + 255) % 510 - 255)
def curve(rng, o, step, off, slide, share):
    h = W // 2; a = walk(rng, h, step); t = np.arange(h)
    xs = np.empty((16, W), np.int64); xs[:, o[:h]] = a; xs[:, o[h:]] = np.clip(a + rng.integers(-off, off + 1, (16, h)), 0, 255)
    cut = rng.random(W) < share
    if share >= 0: cut[h] = True; cut[0:16:3] = True
    nx, pv = rings(o, cut); s = rng.integers(-slide, slide + 1, (2, h)); p = np.empty(W, np.int64)
    p[o[:h]] = o[h + (t + s[0]) % h]; p[o[h:]] = o[(t + s[1]) % h]
    return xs, nx, pv, p
def odd(rng, o, nx, pv, p):
    m = rng.random(W)
    p = np.where(m < 0.03, rng.integers(0, W, W), np.where(m < 0.05, np.arange(W), np.where(m < 0.07, nx, np.where(m < 0.09, pv, p))))
    p[o[0:15:3]] = nx[o[0:15:3]]; p[o[1:15:3]] = pv[o[1:15:3]]
    return p
def links(a):
    return np.stack([gtable(a.reshape(8, N, V)[:, q]) for q in range(N)])
def pack(gs, th):
    xs, nx, pv, p = [np.stack(a) for a in zip(*gs)]
    return {"x": np.ascontiguousarray(xs.reshape(8, 16, N, V).transpose(2, 0, 1, 3)).reshape(N, 128, V).astype(np.int32),
            "nxt": links(nx), "prv": links(pv), "ptn": links(p),
            "th": np.tile(np.repeat(np.asarray(th), 16)[None, :, None], (N, 1, 1)).astype(np.int32)}
def setup_inputs(rng):
    gs, th = [], []
    for g in range(8):
        off = int(rng.integers(4, 13)); step = int(rng.integers(off, 2 * off + 1)); o = rng.permutation(W)
        xs, nx, pv, p = curve(rng, o, step, off, RO, 0.02)
        gs.append((xs, nx, pv, odd(rng, o, nx, pv, p))); th.append(int(rng.integers(4 * off * off, 9 * off * off)))
    return pack(gs, th)
def setup_inputs_ties(rng):
    gs, th = [], []; w = np.arange(W)
    for g in range(8):
        o = rng.permutation(W)
        if g == 6: o = np.ascontiguousarray(w.reshape(N, 2, V // 2).transpose(1, 0, 2)).reshape(-1)
        if g == 7: o = w
        q = int(rng.integers(1, 5)); xs, nx, pv, p = curve(rng, o, 4, 0, 1, -1.0 if g == 5 else 0.02)
        sort = rng.integers(0, 3, W) if g > 1 else np.zeros(W, np.int64)
        u = rng.integers(0, 250, (16, 1)); lo = np.arange(16)[:, None] < 8
        xs = u + q * np.where(sort == 1, lo, np.where(sort == 2, ~lo, False)).astype(np.int64)
        gs.append((xs, nx, pv, p)); th.append((1, 0, 8 * q * q, 8 * q * q + 1, 16 * q * q, 16 * q * q + 1, 8 * q * q, 8 * q * q + 1)[g])
    return pack(gs, th)
def setup_inputs_loops(rng):
    gs, th = [], []; ra, rb, rc = [int(v) for v in rng.permutation(N)[:3]]; w = np.arange(W).reshape(N, V); k = V // 2; c = W - 2 * V; b = W - V
    for g in range(8):
        out = [q for q in range(N) if q != rb and q != rc and (g < 7 or q != ra)]
        few = w[ra] if g == 7 else w[ra][:0]
        o = np.concatenate([rng.permutation(w[out].reshape(-1)), rng.permutation(few), rng.permutation(w[rc]), rng.permutation(w[rb])])
        m = len(out) * V; h = m // 2; t = np.arange(h); j = np.arange(c - m) % 6
        xs = np.empty((16, W), np.int64); xs[:, o] = walk(rng, W, 6)
        xs[:, o[h:m]] = np.clip(xs[:, o[:h]] + rng.integers(-4, 5, (16, h)), 0, 255)
        xs[:, o[c + k:b]] = np.clip(xs[:, o[c:c + k]] + rng.integers(-4, 5, (16, k)), 0, 255)
        cut = rng.random(W) < (1.0, -1.0, 0.5, 0.3, 0.4, 0.05, 0.02, 0.3)[g]
        if g != 1: cut[h] = True
        cut[m] = True; cut[m:c] = (j == 0) | (j == 3) | (j == 5); cut[c:b] = True; cut[b] = True
        if g == 6: cut[1:16] = False
        nx, pv = rings(o, cut); s = rng.integers(-1, 2, (2, h)); p = np.empty(W, np.int64)
        p[o[:h]] = o[h + (t + s[0]) % h]; p[o[h:m]] = o[(t + s[1]) % h]
        i = o[m:c]; u = rng.integers(0, 3, c - m); p[i] = np.where(u == 0, i, np.where(u == 1, nx[i], pv[i]))
        p[o[c:c + k]] = o[c + k:b]; p[o[c + k:b]] = o[c:c + k]; p[o[b:]] = o[rng.integers(0, m, V)]
        if 2 <= g <= 4:
            i = o[0:m:2]; p[i] = np.where(rng.random(h) < 0.7, nx[i], p[i])
            i = o[1:m:2]; p[i] = np.where(rng.random(h) < 0.7, pv[i], p[i])
        if g == 5: p = ra * V + rng.integers(0, V, W)
        if g == 6:
            u = rng.integers(60, 196, (16, 1)); xs = u + rng.integers(-40, 41, (16, W))
            xs[:, o[np.array([5, 20])]] = u; xs[:, o[np.array([3, 4, 6, 7])]] = np.where(u < 128, 255, 0)
            p = np.full(W, o[5], np.int64); p[o[5]] = o[20]
        if g == 7:
            i = o[:m]; p[i] = np.where(rng.random(m) < 0.75, i, p[i])
        gs.append((xs, nx, pv, p)); th.append(10000 if g == 6 else int(rng.integers(300, 4000)))
    return pack(gs, th)
def setup_inputs_ends(rng):
    gs, th = [], []; h = W // 2
    for g in range(8):
        r = 1 + rng.permutation(W - 2); o = np.concatenate([np.array([0]), r[:h - 1], np.array([W - 1]), r[h - 1:]])
        xs, nx, pv, p = curve(rng, o, 4, 0, 0, 0.02)
        if g == 0: p[o[3:15:3]] = nx[o[3:15:3]]; p[o[4:15:3]] = pv[o[4:15:3]]
        xs = 255 * rng.integers(0, 2, (16, W))
        if g == 1:
            nx, pv = rings(o, np.arange(W) % 4 == 0); y = 255 * rng.integers(0, 2, (16, W // 4, 2)); s = rng.integers(0, 3, W)
            xs[:, o] = np.concatenate([y, 255 - y], axis=2).reshape(16, W); p = np.where(s == 0, nx, np.where(s == 1, pv, nx[nx]))
        if g in (2, 3, 7):
            u = 255 * rng.integers(0, 2, (16, 1)); xs[:, o[:h]] = u; xs[:, o[h:]] = 255 - u
        if g == 7: xs[14] = 100; xs[15] = 100 + rng.integers(0, 2, W)
        gs.append((xs, nx, pv, p)); th.append((2 ** 20, 2 ** 20, 1040400, 1040401, 520200, 0, 1, 14 * 255 * 255 + 1)[g])
    return pack(gs, th)
def setup_inputs_near(rng):
    gs, th = [], []; h = W // 2; back = int(rng.integers(0, 2))
    for g in range(8):
        r = np.stack([q * V + rng.permutation(V) for q in range(N)])
        o = np.concatenate([np.ascontiguousarray(r[:, :V // 2].T).reshape(-1), np.ascontiguousarray(np.roll(r[:, V // 2:], N // 2, axis=0).T).reshape(-1)])
        off = int(rng.integers(2, 6)); a = walk(rng, h, 16 * off)
        xs = np.empty((16, W), np.int64); xs[:, o[:h]] = a; xs[:, o[h:]] = np.clip(a + rng.integers(-off, off + 1, (16, h)), 0, 255)
        cut = (rng.random(W) < 0.04) & (np.arange(W) % N == 0); cut[h] = True
        nx, pv = rings(o, cut); mate = np.empty(W, np.int64); mate[o[:h]] = o[h:]; mate[o[h:]] = o[:h]
        gs.append((xs, nx, pv, pv[mate] if back else nx[mate])); th.append(int(rng.integers(17 * off * off, 40 * off * off)))
    return pack(gs, th)
def setup_inputs_spread(rng):
    gs, th = [], []
    for g in range(8):
        o = rng.permutation(W); xs, nx, pv, p = curve(rng, o, int(rng.integers(2, 40)), int(rng.integers(0, 30)), RO, 0.02)
        xs = np.where(rng.random(W) < 0.1, rng.integers(0, 256, (16, W)), xs >> rng.integers(0, 7, (16, 1)))
        gs.append((xs, nx, pv, odd(rng, o, nx, pv, p))); th.append(int(2.0 ** (20 * rng.random())))
    return pack(gs, th)
def joined(a):
    return np.ascontiguousarray(np.stack([gentries(b) for b in a]).transpose(1, 0, 2)).reshape(8, W).astype(np.int64)
def check_inputs(d):
    bad = []
    for k, hi in (("x", 255), ("nxt", W - 1), ("prv", W - 1), ("ptn", W - 1), ("th", 2 ** 20)):
        if np.min(d[k]) < 0 or np.max(d[k]) > hi: bad.append("range of " + k)
    t = d["th"].reshape(N, 8, 16)
    if np.any(t != t[:1, :, :1]): bad.append("th alike on all ranks and in a group")
    if "range of nxt" not in bad and "range of prv" not in bad:
        if np.any(np.take_along_axis(joined(d["prv"]), joined(d["nxt"]), 1) != np.arange(W)[None, :]): bad.append("prv is the inverse of nxt")
    return bad
def at(a, i):
    return np.take_along_axis(a, i, 1)
def points(a, i):
    return np.take_along_axis(a, i[:, None, :], 2)
def reference(x, nxt, prv, ptn, th):
    z = np.ascontiguousarray(x.astype(np.int64).reshape(N, 8, 16, V).transpose(1, 2, 0, 3)).reshape(8, 16, W)
    nx = joined(nxt); pv = joined(prv); p = joined(ptn); t = th[0].astype(np.int64).reshape(8, 16)[:, :1]
    me = np.arange(W)[None, :]
    for rnd in range(RO):
        a = at(nx, p); b = at(pv, p)
        c = np.stack([p, a, b] + ([at(nx, a), at(pv, b)] if HOP == 2 else []))
        d = np.stack([np.add.reduce((z - points(z, k)) ** 2, axis=1) for k in c])
        d = np.where((c == me) | (c == nx) | (c == pv), 2 ** 21, d)
        k = np.argmin(d, axis=0)[None]
        p = np.take_along_axis(c, k, 0)[0]; e = np.take_along_axis(d, k, 0)[0]
        swap = (at(p, p) == me) & (e < t)
        nx, pv = np.where(swap, at(nx, p), nx), np.where(at(swap, pv), at(p, pv), pv)
        z = (2 * z + points(z, nx) + points(z, pv)) >> 2
    return {"yx": np.ascontiguousarray(z.reshape(8, 16, N, V).transpose(2, 0, 1, 3)).reshape(N, 128, V).astype(np.float32),
            "yn": links(nx).astype(np.float32), "yv": links(pv).astype(np.float32), "yp": links(p).astype(np.float32)}

@@ -1,0 +1,628 @@
+from concourse.bass import DstId, RemoteDMATransfer
+from concourse.mybir import AluOpType, AxisListType, ActivationFunctionType
+
+N, V, W = 4, 1536, 6144
+ZOFF = 3079.5
+IOFF = 3072.0
+M16 = 1.5 * 2 ** 27
+M1 = 1.5 * 2 ** 23
+BIG = float(2 ** 20)
+OPT = {"dq": "ssss", "sp": "aaaavavavavavava", "g2": 6, "w2": 12, "gp": "vvaa", "c0": 24, "c2": 0}
+
+F, B, I, U = "float32", "bfloat16", "int32", "uint16"
+SCRATCH = {
+    "ZT": ("sbuf", [128, W], B), "NP": ("sbuf", [128, W], B), "QT": ("sbuf", [128, W], B),
+    "ZA": ("sbuf", [128, V], B), "ZN": ("sbuf", [128, V], B),
+    "XI": ("sbuf", [128, V], I), "LI": ("sbuf", [128, 288], I), "TI": ("sbuf", [128, 4], I),
+    "LZ": ("sbuf", [128, 288], F), "LT": ("sbuf", [128, 288], B), "LC": ("sbuf", [128, 288], B),
+    "XS": ("sbuf", [128, V], B), "LAND": ("sbuf", [128, V], B),
+    "SX": ("sbuf", [128, 384], B), "XL": ("sbuf", [128, 4, 4, 24], B),
+    "SP": ("sbuf", [128, 384], B), "PL": ("sbuf", [128, 4, 4, 24], B),
+    "XQ": ("sbuf", [128, 4, 4, 24], B), "XN": ("sbuf", [128, 4, 4, 24], B), "DT": ("sbuf", [128, 640], F),
+    "R0": ("sbuf", [128, V], B), "R1": ("sbuf", [128, V], B), "R2": ("sbuf", [128, V], B),
+    "GN": ("sbuf", [128, V], B), "GP": ("sbuf", [128, V], B),
+    "DF": ("sbuf", [128, 5 * V], B), "SQ": ("sbuf", [128, 5 * V], F),
+    "WF": ("sbuf", [128, 96 * 90], F), "WB": ("sbuf", [128, 96 * 40], B), "WU": ("sbuf", [128, 96 * 32], U),
+    "COL": ("sbuf", [128, 8], F), "WI": ("sbuf", [128, 4], F),
+    "ZB": ("sbuf", [128, 576], B), "ZF": ("sbuf", [128, 192], F), "ONE": ("sbuf", [128, 144], F), "CM": ("sbuf", [128, 384], B),
+    "MC": ("sbuf", [128, 576], B), "ME": ("sbuf", [128, 512], B), "PT": ("sbuf", [128, 128], B),
+    "DM": ("sbuf", [128, 4 * 224], B), "BM": ("sbuf", [128, 4 * 144], B), "MD": ("sbuf", [128, 144], F),
+    "REP": ("sbuf", [128, 512], B), "DG": ("sbuf", [128, 640], B), "PM": ("sbuf", [128, 256], B),
+    "MQ": ("sbuf", [128, 288], B), "IDF": ("sbuf", [128, 128], F), "VR": ("sbuf", [128, 128], F), "MH": ("sbuf", [128, 768], F),
+    "LS": ("sbuf", [128, 4, 4, 24], U), "LL": ("sbuf", [128, 384], U), "LO": ("sbuf", [128, 384], F),
+    "ZS": ("sbuf", [128, V], B), "ZL": ("sbuf", [128, V], B), "ZO": ("sbuf", [128, V], F),
+}
+for _i in range(8):
+    SCRATCH["P%d" % _i] = ("psum", [128, 512], F)
+NDMA = 52
+SEMAPHORES = ["qg", "qv", "qa", "qt", "sent"] + ["d%d" % i for i in range(NDMA)] + ["arrl", "arrp", "arrm"] + \
+    ["arrx%d" % i for i in range(N)] + ["arrz%d" % i for i in range(N)]
+
+ADD, SUB, MUL, MIN = AluOpType.add, AluOpType.subtract, AluOpType.mult, AluOpType.min
+EQ, NE, LT, GE = AluOpType.is_equal, AluOpType.not_equal, AluOpType.is_lt, AluOpType.is_ge
+COPY, SQUARE = ActivationFunctionType.Copy, ActivationFunctionType.Square
+
+
+def rank_program(g, core, T, topo):
+    me = T.rank_of(core)
+    if me is None:
+        return
+    cores = T.cores
+    near = [r for r in range(N) if r != me and cores[r] in topo.cores_of(core)]
+    far = [r for r in range(N) if r != me and r not in near]
+    far.sort(key=lambda r: topo.die(cores[r]) != topo.die(core))
+
+    def bits(es):
+        return sum(1 << e for e in es)
+
+    def mask_for(src, dst):
+        cs = cores[src]
+        fr = [r for r in range(N) if r != src and cores[r] not in topo.cores_of(cs)]
+        off = topo.engines(cs, cores[fr[0]])
+        if dst in fr:
+            h = len(off) // len(fr)
+            i = fr.index(dst)
+            return off[i * h:(i + 1) * h]
+        return [e for e in topo.engines(cs, cores[dst]) if e not in off]
+
+    eng = {"g": g, "v": g.vector, "a": g.scalar, "t": g.tensor, "s": g.sync}
+    qsem = {"g": "qg", "v": "qv", "a": "qa", "t": "qt"}
+    count = {}
+    seen = {q: {} for q in eng}
+    hist = {}
+    ndma = [0]
+
+    def A(name, lo=None, hi=None, step=1, tag=None):
+        if lo is None:
+            return (T[name][:], name, 0, 1 << 20, tag)
+        ap = T[name][:, lo:hi] if step == 1 else T[name][:, lo:hi:step]
+        return (ap, name, lo, hi, tag)
+
+    def X(ap, name, tag=None):
+        return (ap, name, 0, 1 << 20, tag)
+
+    def blk(name, r, w=384):
+        return A(name, w * r, w * r + w)
+
+    def wait(q, tok):
+        if seen[q].get(tok[0], 0) < tok[1]:
+            eng[q].wait_ge(T.sem[tok[0]], tok[1])
+            seen[q][tok[0]] = tok[1]
+
+    def order(q, reads, writes, tok):
+        need = {}
+        for views, wr in ((reads, False), (writes, True)):
+            for (_ap, name, lo, hi, tag) in views:
+                bank = SCRATCH[name][0] == "psum"
+                for (l2, h2, tag2, w2, tok2, q2) in hist.get(name, []):
+                    if bank:
+                        if q2 == q and (q == "t" or not (wr or w2)):
+                            continue
+                    elif not (wr or w2) or l2 >= hi or lo >= h2 or (tag is not None and tag2 is not None and tag != tag2):
+                        continue
+                    need[tok2[0]] = max(need.get(tok2[0], 0), tok2[1])
+        for s in need:
+            wait(q, (s, need[s]))
+        for views, wr in ((reads, False), (writes, True)):
+            for (_ap, name, lo, hi, tag) in views:
+                h = hist.setdefault(name, [])
+                if wr and tag is None and SCRATCH[name][0] != "psum":
+                    h[:] = [e for e in h if not (lo <= e[0] and e[1] <= hi)]
+                if SCRATCH[name][0] == "psum":
+                    h[:] = [e for e in h if e[5] == q and e[3] and not wr]
+                h.append((lo, hi, tag, wr, tok, q))
+
+    def op(q, call, reads, writes):
+        s = qsem[q]
+        tok = (s, count.get(s, 0) + 1)
+        order(q, reads, writes, tok)
+        call().then_inc(T.sem[s], 1)
+        count[s] = tok[1]
+
+    def dma(q, out, in_, reads, writes):
+        s = "d%d" % ndma[0]
+        ndma[0] += 1
+        order(q, reads, writes, (s, 16))
+        eng[q].dma_start(out, in_).then_inc(T.sem[s], 16)
+        count[s] = 16
+
+    def arrives(view, sem, n):
+        count[sem] = n
+        hist.setdefault(view[1], []).append((view[2], view[3], view[4], True, (sem, n), "r"))
+
+    def send(items):
+        trs, n = [], 0
+        for (r, src, dst, sem) in items:
+            rid, pid = topo.addr(cores[r], core)
+            es = mask_for(me, r)
+            n += len(es)
+            trs.append(RemoteDMATransfer(dst_ids=[DstId(rid=rid, pnc=pid)], dma_engine_mask=bits(es), remote_sem=T.sem[sem],
+                                         src=src[0], dst=dst))
+        order("g", [it[1] for it in items], [], ("sent", 1 << 20))
+        g.remote_dma_fused(trs, local_sem=T.sem.sent)
+        count["sent"] = count.get("sent", 0) + n
+
+    def ts(out, in0, s1, s2, o0, o1=None, extra=()):
+        if o1 is None:
+            op("v", lambda: g.vector.tensor_scalar(out[0], in0[0], s1, None, o0), [in0] + list(extra), [out])
+        else:
+            op("v", lambda: g.vector.tensor_scalar(out[0], in0[0], s1, s2, o0, o1), [in0] + list(extra), [out])
+
+    def tt(out, a, b, o):
+        op("v", lambda: g.vector.tensor_tensor(out[0], a[0], b[0], o), [a, b], [out])
+
+    def cp(q, out, in_):
+        if q == "v":
+            op("v", lambda: g.vector.tensor_copy(out[0], in_[0]), [in_], [out])
+        else:
+            op("a", lambda: g.scalar.activation(out[0], in_[0], COPY), [in_], [out])
+
+    def fill(view, val):
+        op("v", lambda: g.vector.memset(view[0], val), [], [view])
+
+    def mm(out, lhsT, rhs, start, stop):
+        op("t", lambda: g.tensor.matmul(out[0], lhsT[0], rhs[0], start, stop), [lhsT, rhs], [out])
+
+    def sel(out, in_, pattern, cmp, val, base, cm=1):
+        op("g", lambda: g.affine_select(out[0], in_[0], pattern, cmp, val, base, cm), [in_], [out])
+
+    def iota(out, pattern, base):
+        op("g", lambda: g.iota(out[0], pattern, base, 0, allow_small_or_imprecise_dtypes=True), [], [out])
+
+    def gather(q, win, offs, out, lo, hi):
+        o, w, d = A("WU", 96 * offs + lo, 96 * offs + hi), A(win, 0, W), A(out, 16 * lo, 16 * hi)
+        if q == "v":
+            op("v", lambda: g.vector.tensor_copy(d[0], w[0].indirect(o[0])), [o, w], [d])
+        else:
+            op("a", lambda: g.scalar.activation(d[0], w[0].indirect(o[0]), COPY), [o, w], [d])
+
+    def gather2(win, offs, out):
+        gather("a", win, offs, out, 48, 96)
+        gather("v", win, offs, out, 0, 48)
+
+    slots = {"WF": [0], "WB": [0], "WU": [0]}
+
+    def new(buf):
+        slots[buf][0] += 1
+        return slots[buf][0] - 1
+
+    def wf(i):
+        return blk("WF", i, 96)
+
+    def wb(i):
+        return blk("WB", i, 96)
+
+    def wu(i):
+        return blk("WU", i, 96)
+
+    def ps(b, lo=0, n=96):
+        return A("P%d" % b, lo, lo + n)
+
+    def dg(i):
+        return blk("DG", i, 128)
+
+    NXZ, NXI, PVZ, PVI = 0, 1, 2, 3
+
+    def wrap(rows, m, bank):
+        for c in range(16):
+            mm(ps(bank), A("BM", 144 * m + 15 - c, 144 * m + 143 - c), A(rows, c, V, 16), c == 0, c == 15)
+
+    def to_u(src, add):
+        i = new("WU")
+        ts(wu(i), src, add, None, ADD)
+        return i
+
+    def to_f(src):
+        i = new("WF")
+        cp("v", wf(i), src)
+        return i
+
+    def split(v):
+        t, c = new("WB"), new("WB")
+        ts(wb(t), v, M16, M16, ADD, SUB)
+        tt(wb(c), v, wb(t), SUB)
+        return t, c
+
+    def iform_mm(pc, bank):
+        mm(ps(bank), dg(0), wb(pc[0]), True, False)
+        mm(ps(bank), dg(1), wb(pc[1]), False, True)
+
+    def mc(r, slot):
+        return A("MC", 128 * r + 48 - 16 * slot, 128 * r + 176 - 16 * slot)
+
+    def flatten(buf, rows, win, step):
+        for k in range(4):
+            dma(OPT["dq"][k], T[win][32 * k:32 * k + 32:step, :], T[buf][0:rows], [A(buf)], [A(win, tag=k)])
+
+    def table_out(buf, rows, banks):
+        for k in (0, 2, 1, 3):
+            b = "P%d" % banks[k // 2]
+            cp("va"[k // 2], X(T[buf][0:rows, :, k, :], buf, tag=k), X(T[b][0:rows, 96 * (k % 2):96 * (k % 2) + 96], b))
+
+    def fsel(base, cond, delta, out=None):
+        a = new("WF")
+        tt(wf(a), delta, cond, MUL)
+        if out is None:
+            b = new("WF")
+            tt(wf(b), base, wf(a), ADD)
+            return b
+        tt(out, base, wf(a), ADD)
+
+    for j, name in enumerate(("nxt", "prv", "ptn")):
+        dma("s", T.LI[:, 96 * j:96 * j + 96], T[name][:], [], [blk("LI", j, 96)])
+    for r in far + near + [me]:
+        dma("a", blk("XI", r)[0], T.x[32 * r:32 * r + 32, :], [], [blk("XI", r)])
+    for k in range(4):
+        dma("s", T.TI[32 * k:32 * k + 32, 0:1], T.th[32 * me:32 * me + 32, :], [], [A("TI", tag=k)])
+    for r in near + far:
+        arrives(blk("LAND", r), "arrx%d" % r, len(mask_for(r, me)))
+        arrives(blk("ZL", r), "arrz%d" % r, len(mask_for(r, me)))
+    nl = sum(len(mask_for(r, me)) for r in near + far)
+    arrives(A("XL", tag="far"), "arrl", nl)
+    arrives(A("PL", tag="far"), "arrp", nl)
+    arrives(A("LL", tag="far"), "arrm", nl)
+
+    def dmaster(m, pieces):
+        v = blk("DM", m, 224)
+        for n, piece in enumerate(pieces):
+            sel(v, v if n else A("ZB", 0, 224), [[-256, 7], [-64, 2], [-1, 16]], NE, 1.0, 768 - 16 * piece)
+
+    def bmaster(m, row, w0, w1):
+        v = blk("BM", m, 144)
+        sel(v, A("ZB", 0, 144), [[-16, 9], [-256, 16]], NE, w0, 3840 - row)
+        sel(v, v, [[-16, 9], [-256, 16]], NE, w1, 3840 - row - 8)
+
+    fill(A("ZB"), 0.0)
+    fill(A("NP", 0, 2048), 0.0)
+    for b in range(4):
+        fill(X(T.WI[32 * b:32 * b + 32, 0:1], "WI", tag=b), 384.0 if b % 2 else 1.0 / 16)
+    cp("a", A("NP", 2048, 4096), A("NP", 0, 2048))
+    sel(A("MC"), A("ZB"), [[-16, 9], [-256, 4], [-1, 16]], NE, 1.0, 768)
+    dmaster(NXZ, (0, 2))
+    bmaster(NXI, 0, 1.0 / 16, 384.0)
+    sel(A("ME"), A("ZB", 0, 512), [[-1, 4], [0, 4], [-4, 32]], NE, 1.0, 0)
+
+    for lo, hi in ((0, 192), (192, 288)):
+        ts(A("LZ", lo, hi), A("LI", lo, hi), -ZOFF, None, ADD)
+        ts(A("LT", lo, hi), A("LZ", lo, hi), M16, M16, ADD, SUB)
+        tt(A("LC", lo, hi), A("LZ", lo, hi), A("LT", lo, hi), SUB)
+    for r in range(N):
+        for slot, (src, j) in enumerate((("LT", 0), ("LT", 1), ("LC", 0), ("LC", 1))):
+            mm(ps(0, 96 * r), mc(r, slot), blk(src, j, 96), slot == 0, slot == 3)
+    for r in range(N):
+        mm(ps(1, 96 * r), mc(r, 0), blk("LT", 2, 96), True, False)
+        mm(ps(1, 96 * r), mc(r, 2), blk("LC", 2, 96), False, True)
+    cp("a", A("SX"), ps(0, 0, 384))
+    cp("a", A("SP"), ps(1, 0, 384))
+    cp("a", A("NP", 4096, W), A("NP", 0, 2048))
+    send([(r, blk("SX", r, 96), T.XL[:, me], "arrl") for r in far + near])
+    send([(r, blk("SP", r, 96), T.PL[:, me], "arrp") for r in far + near])
+    for r in far + near:
+        cp("v", blk("XS", r), blk("XI", r))
+    send([(r, blk("XS", r), blk("LAND", me)[0], "arrx%d" % me) for r in far + near])
+    cp("v", blk("LAND", me), blk("XI", me))
+    cp("v", X(T.XL[:, me], "XL", tag="own"), blk("SX", me, 96))
+    cp("v", X(T.PL[:, me], "PL", tag="own"), blk("SP", me, 96))
+    flatten("XL", 128, "NP", 4)
+
+    wi = X(T.WI[:, 0:1], "WI")
+    ts(blk("DM", NXI, 224), blk("DM", NXZ, 224), wi[0], None, MUL, extra=[wi])
+    fill(A("ZF"), 0.0)
+    fill(A("ONE"), 1.0)
+    fill(A("CM"), -1.5)
+    cp("v", A("COL", 2, 3), A("TI", 0, 1))
+    th = A("COL", 2, 3)
+    sel(A("PT"), A("ZB", 0, 128), [[-1, 4], [-4, 32]], NE, 1.0, 0)
+    ts(blk("BM", NXZ, 144), blk("BM", NXI, 144), 0.0, None, NE)
+    dmaster(PVZ, (1, 3))
+    iota(A("VR"), [[384, 4], [0, 2], [1, 16]], 0)
+    sel(A("VR"), A("VR"), [[-1, 128]], EQ, 0.0, 0)
+    ident0, ident = new("WF"), new("WF")
+    iota(wf(ident0), [[1536, 4], [16, 24]], 0)
+    bmaster(PVI, 4, 1.0 / 16, 384.0)
+    sel(A("MD"), A("ONE"), [[-16, 9], [256, 16]], GE, 0.0, -3840)
+    sel(A("MD"), A("MD"), [[16, 9], [0, 16]], GE, 0.0, 15, -1)
+    sel(dg(4), A("ZB", 0, 128), [[-1, 128]], NE, BIG, 0)
+    sel(A("IDF"), A("ZF", 0, 128), [[-1, 128]], NE, 1.0, 0)
+    sel(A("MQ"), A("ZB", 0, 288), [[-16, 9], [-256, 2], [-1, 16]], NE, 1.0, 256)
+    for i, w in ((0, 1.0 / 16), (1, 384.0), (2, 0.25), (3, 0.5)):
+        sel(dg(i), A("ZB", 0, 128), [[-1, 128]], NE, w, 0)
+    sel(A("REP"), A("ZB", 0, 512), [[-32, 4], [0, 4], [-1, 32]], NE, 1.0, 0)
+    for i, w in enumerate((0.25, 0.5)):
+        sel(blk("PM", i, 128), A("ZB", 0, 128), [[-1, 32], [-32, 4]], NE, w, 0)
+    for k in range(4):
+        sel(blk("MH", k, 192), A("ZF"), [[-256, 6], [-1, 32]], NE, 1.0, 512 - 32 * k)
+
+    rot = [0]
+
+    def spread(lhsT, rhs, out, banks, q):
+        b = banks[rot[0] % len(banks)]
+        mm(ps(b, 0, 384), lhsT, rhs, True, True)
+        cp(q, out, ps(b, 0, 384))
+        rot[0] += 1
+
+    def source(r):
+        for a in range(5):
+            spread(blk("ME", a, 128) if a < 4 else A("PT"), blk("LAND", r), blk("ZT", 4 * r + a) if a < 4 else blk("ZA", r),
+                   (3, 4, 5, 6, 7, 2, 0) if r == far[1] else (3, 4, 5, 6, 7), "va"[rot[0] % 2])
+
+    def own_list(m, buf, bank):
+        for k in range(4):
+            mm(ps(bank), A("DM", 224 * m + 96 - 32 * k, 224 * m + 224 - 32 * k), X(T[buf][:, :, k, :], buf), k == 0, k == 3)
+
+    st = {}
+
+    def equal(a, b):
+        e = new("WB")
+        tt(wb(e), a, wf(b), EQ)
+        return e
+
+    KEY = (4, 4, 5, 6, 4)
+    DTB = ("P3", "P1", "P3", "P1", "P3")
+
+    def key(k):
+        return ps(KEY[k], 96 * (k % 2))
+
+    def diff(k, offs, zown, lo=0, hi=96):
+        o, w = A("WU", 96 * offs + lo, 96 * offs + hi), A("ZT", 0, W)
+        d, z = A("DF", V * k + 16 * lo, V * k + 16 * hi), A(zown, 16 * lo, 16 * hi)
+        op("v", lambda: g.vector.tensor_tensor(d[0], w[0].indirect(o[0]), z[0], SUB), [o, w, z], [d])
+
+    def square(k, lo=0, hi=96):
+        d, s = A("DF", V * k + 16 * lo, V * k + 16 * hi), A("SQ", V * k + 16 * lo, V * k + 16 * hi)
+        op("a", lambda: g.scalar.activation(s[0], d[0], SQUARE), [d], [s])
+
+    def dist(k):
+        for c in range(16):
+            mm(X(T[DTB[k]][0:96, c:128:16], DTB[k]), A("SQ", V * k + c, V * k + V, 16), A("MD", 15, 128, 16), True, True)
+
+    def turn(k, flags):
+        d = (T.DT[0:96, 128 * k:128 * k + 128], "DT", 128 * k, 128 * k + 128, None)
+        cp("a", d, X(T[DTB[k]][0:96, 0:128], DTB[k]))
+        for n, e in enumerate(flags):
+            mm(key(k), dg(4), wb(e), n == 0, False)
+        mm(key(k), d, X(T.IDF[0:96, 0:96], "IDF"), False, True)
+
+    def choose(c, flags):
+        least, best, d, qb, dp, q = new("WF"), ps(7, 0), ps(7, 96), ps(7, 192), ps(7, 288), ps(7, 384)
+        ts(wf(least), key(0), BIG, None, MIN)
+        for k in range(1, 4):
+            lt, m = new("WF"), new("WF")
+            old = best if k > 1 else wf(c[0])
+            tt(wf(lt), key(k), wf(least), LT)
+            tt(d, wf(c[k]), old, SUB)
+            tt(wf(m), key(k), wf(least), MIN)
+            fsel(old, wf(lt), d, best)
+            least = m
+            if k == 1:
+                turn(4, flags)
+        ok, mt, lq, lp = [new("WF") for _ in range(4)]
+        ts(wf(ok), wf(least), th[0], None, LT, extra=[th])
+        tt(d, best, wf(ident), SUB)
+        ts(wf(mt), wf(least), th[0], None, MIN, extra=[th])
+        fsel(wf(ident), wf(ok), d, qb)
+        tt(dp, wf(c[4]), best, SUB)
+        tt(d, wf(c[4]), qb, SUB)
+        tt(wf(lq), key(4), wf(mt), LT)
+        fsel(qb, wf(lq), d, q)
+        return q, (best, least, lp, dp)
+
+    def begin():
+        source(me)
+        v, o = A("VR"), A("COL", 1, 2)
+        op("v", lambda: g.vector.tensor_reduce(o[0], v[0], AxisListType.X, ADD), [v], [o])
+        ts(wf(ident), wf(ident0), T.COL[:, 1:2], -ZOFF, ADD, ADD, extra=[o])
+        ts(blk("DM", PVI, 224), blk("DM", PVZ, 224), wi[0], None, MUL, extra=[wi])
+        own_list(NXZ, "XL", 2)
+        own_list(PVZ, "XL", 1)
+        own_list(PVI, "XL", 0)
+        st["nx"], st["pv"], st["pvi"] = to_f(ps(2)), to_f(ps(1)), to_u(ps(0), IOFF)
+        own_list(NXI, "PL", 0)
+        own_list(NXZ, "PL", 1)
+        pi, st["pz"], st["p"] = to_u(ps(0), IOFF), to_u(ps(1), ZOFF), to_f(ps(1))
+        source(near[0])
+        gather2("NP", pi, "R0")
+        ts(blk("BM", PVZ, 144), blk("BM", PVI, 144), 0.0, None, NE)
+        source(far[0])
+        source(far[1])
+        wrap("R0", NXI, 1)
+        dma("s", T.QT[:], T.ZT[:], [A("ZT")], [A("QT")])
+
+    def slide(zown, cut):
+        wrap("R0", NXZ, 0)
+        wrap("R0", PVI, 2)
+        if cut:
+            diff(0, st["pz"], zown, 0, cut)
+        c1i = to_u(ps(1), IOFF)
+        wrap("R0", PVZ, 1)
+        gather("a", "NP", c1i, "R1", 0, 96)
+        diff(0, st["pz"], zown, cut, 96)
+        square(0)
+        c1z, c2i = to_u(ps(0), ZOFF), to_u(ps(2), IOFF)
+        gather("a", "NP", c2i, "R2", 0, 48)
+        c1 = to_f(ps(0))
+        wrap("R1", NXZ, 0)
+        dist(0)
+        diff(1, c1z, zown)
+        square(1)
+        c2z, c2, e2 = to_u(ps(1), ZOFF), to_f(ps(1)), equal(ps(1), ident)
+        e0, e1 = equal(wf(st["p"]), ident), equal(wf(c1), ident)
+        dist(1)
+        turn(0, (e2, e0, e1))
+        gather("a", "NP", c2i, "R2", 48, 96)
+        wrap("R2", PVZ, 2)
+        diff(2, c2z, zown)
+        square(2)
+        c3z, c3, e3, e3p = to_u(ps(0), ZOFF), to_f(ps(0)), equal(ps(0), ident), equal(ps(0), st["pv"])
+        dist(2)
+        turn(1, (e0, e1, e3))
+        for lo in (0, 48):
+            diff(3, c3z, zown, lo, lo + 48)
+            square(3, lo, lo + 48)
+        c4z, c4, e4, e4n = to_u(ps(2), ZOFF), to_f(ps(2)), equal(ps(2), ident), equal(ps(2), st["nx"])
+        turn(2, (e4, e2, e0))
+        dist(3)
+        for lo in (0, 48):
+            diff(4, c4z, zown, lo, lo + 48)
+            square(4, lo, lo + 48)
+        turn(3, (e1, e3, e3p))
+        dist(4)
+        return [st["p"], c1, c2, c3, c4], (e4n, e4, e2)
+
+    def list_mm(i, row, stop):
+        for k in range(4):
+            o = 192 * k + 64 - 32 * row
+            mm(ps(3, 96 * k), A("MH", o, o + 128), wf(i), False, stop and k == 3)
+
+    def swap_smooth(c, flags, zown, last):
+        blocks = far + near + [me] if last else [0, 1, 2, 3]
+        quarter, half = (blk("PM", 0, 128), blk("PM", 1, 128)) if last else (dg(2), dg(3))
+
+        def term(n, buf, stop):
+            mm(ps(4 + n, 0, 384), quarter, blk(buf, blocks[n]), False, stop)
+
+        def part(qn, offs, buf, n):
+            gather(qn, "ZT", offs, buf, 24 * blocks[n], 24 * blocks[n] + 24)
+
+        def rounded(buf, n):
+            ts(blk(buf, blocks[n]), ps(4 + n, 0, 384), M1, M1, ADD, SUB)
+
+        def np_mm(pc, slot, stop):
+            for k in range(4):
+                for piece in range(2):
+                    mm(ps((1, 3)[k // 2], 96 * (k % 2)), mc(k, slot + 2 * piece), wb(pc[piece]), False, stop and k % 2 == 1 and piece == 1)
+
+        q, pend = choose(c, flags)
+        qp = split(q)
+        for k in range(4):
+            for piece in range(2):
+                b, o = "P%d" % (k // 2), 64 * k + 16 - 16 * piece
+                mm(X(T[b][0:64, 96 * (k % 2):96 * (k % 2) + 96], b), A("MQ", o, o + 64), wb(qp[piece]), piece == 0, piece == 1)
+        iform_mm(qp, 2)
+        best, least, lp, dp = pend
+        tt(wf(lp), key(4), wf(least), LT)
+        table_out("XQ", 64, (0, 1))
+        flatten("XQ", 64, "QT", 8)
+        qi = to_u(ps(2), IOFF)
+        gather2("NP", qi, "R0")
+        p = fsel(best, wf(lp), dp)
+        for n in range(4):
+            if n == 3:
+                wrap("R0", NXZ, 2)
+            mm(ps(4 + n, 0, 384), half, blk(zown, blocks[n]), True, False)
+            mm(ps(4 + n, 0, 384), quarter, A("CM"), False, False)
+        if not last:
+            pp = split(wf(p))
+            iform_mm(pp, 3)
+        dn, da, sw, sv = [new("WF") for _ in range(4)]
+        gather2("QT", st["pvi"], "R2")
+        wrap("R2", NXI, 0)
+        tt(wf(dn), ps(2), wf(st["nx"]), SUB)
+        gather2("QT", qi, "R1")
+        wrap("R1", NXZ, 1)
+        ai = to_u(ps(0), IOFF)
+        gather2("QT", ai, "R0")
+        wrap("R2", NXZ, 2)
+        wrap("R0", NXZ, 0)
+        tt(wf(sw), ps(1), wf(ident), EQ)
+        nx = fsel(wf(st["nx"]), wf(sw), wf(dn))
+        nz = to_u(wf(nx), ZOFF)
+        for n in range(3 if last else 4):
+            part("a", nz, "GN", n)
+        if last:
+            mm(ps(3, 0, 384), A("ZB", 0, 128), A("ZB", 0, 384), True, False)
+            list_mm(p, 2, False)
+            for n in range(3):
+                term(n, "GN", False)
+        else:
+            st["pi"] = to_u(ps(3), IOFF)
+            npc = split(wf(nx))
+            for b in (1, 3):
+                mm(ps(b, 0, 192), A("ZB", 0, 128), A("ZB", 0, 192), True, False)
+            np_mm(npc, 0, False)
+        tt(wf(da), ps(2), wf(st["pv"]), SUB)
+        tt(wf(sv), ps(0), wf(st["pv"]), EQ)
+        pv = fsel(wf(st["pv"]), wf(sv), wf(da))
+        vz = to_u(wf(pv), ZOFF)
+        if last:
+            land = blk("ZL", me)[0]
+            part("v", vz, "GP", 0)
+            part("a", vz, "GP", 1)
+            part("a", vz, "GP", 2)
+            part("a", nz, "GN", 3)
+            part("a", vz, "GP", 3)
+            for n in range(2):
+                term(n, "GP", True)
+                rounded("ZS", n)
+            send([(r, blk("ZS", r), land, "arrz%d" % me) for r in far])
+            list_mm(pv, 1, False)
+            term(2, "GP", True)
+            list_mm(nx, 0, True)
+            term(3, "GN", False)
+            term(3, "GP", True)
+            rounded("ZS", 2)
+            for k in range(4):
+                ts(X(T.LS[:, :, k, :], "LS", tag=k), ps(3, 96 * k), ZOFF, None, ADD)
+            send([(r, blk("ZS", r), land, "arrz%d" % me) for r in near])
+            send([(r, X(T.LS[:, r], "LS"), blk("LL", me, 96)[0], "arrm") for r in far + near])
+            rounded("ZO", 3)
+            return
+        gp = OPT["gp"]
+        banks = (0, 2, 4, 0, 5, 2, 6, 4, 7, 0, 5, 2, 6, 4, 7, 0)
+        rot[0] = 0
+
+        def spreads(lo, hi):
+            for n in range(lo, hi):
+                spread(blk("REP", n % 4, 128), blk("ZN", n // 4), blk("ZT", n), banks, OPT["sp"][n])
+
+        vpc = split(wf(pv))
+        np_mm(vpc, 1, True)
+        part(gp[0], vz, "GP", 0)
+        table_out("XN", 128, (1, 3))
+        flatten("XN", 128, "NP", 4)
+        for n in range(1, 4):
+            part(gp[n], vz, "GP", n)
+        for n in range(4):
+            term(n, "GN", False)
+        for n in range(2):
+            term(n, "GP", True)
+        iform_mm(vpc, 3)
+        rounded("ZN", 0)
+        spreads(0, 2)
+        for n in range(2, 4):
+            term(n, "GP", True)
+        spreads(2, 4)
+        for n in range(1, 4):
+            rounded("ZN", n)
+        st["nx"], st["pv"], st["p"] = nx, pv, p
+        st["pz"], st["pvi"] = to_u(wf(p), ZOFF), to_u(ps(3), IOFF)
+        spreads(4, OPT["g2"])
+        gather2("NP", st["pi"], "R0")
+        spreads(OPT["g2"], OPT["w2"])
+        wrap("R0", NXI, 1)
+        spreads(OPT["w2"], 16)
+
+    begin()
+    cands, flags = slide("ZA", OPT["c0"])
+    swap_smooth(cands, flags, "ZA", False)
+    cands, flags = slide("ZN", OPT["c2"])
+    swap_smooth(cands, flags, "ZN", True)
+
+    def out_lists(r):
+        for row, name in enumerate(("yn", "yv", "yp")):
+            dma("s", T[name][32 * r:32 * r + 32, :], T.LO[32 * row:32 * row + 32, 96 * r:96 * r + 96], [blk("LO", r, 96)], [])
+
+    def out_points(r, qn):
+        dma(qn, T.yx[32 * r:32 * r + 32, :], blk("ZO", r)[0], [blk("ZO", r)], [])
+
+    out_points(me, "a")
+    cp("v", blk("LO", me, 96), X(T.LS[:, me], "LS"))
+    out_lists(me)
+    for r, qn in ((near[0], "a"), (far[0], "a"), (far[1], "v")):
+        cp(qn, blk("ZO", r), blk("ZL", r))
+        out_points(r, "a" if qn == "a" else "s")
+    for r in near + far:
+        cp("v", blk("LO", r, 96), blk("LL", r, 96))
+        out_lists(r)
+    for s in count:
+        wait("g", (s, count[s]))

@@ -7,40 +7,67 @@ IOFF = 3072.0
 M16 = 1.5 * 2 ** 27
 M1 = 1.5 * 2 ** 23
 BIG = float(2 ** 20)
-OPT = {"dq": "ssss", "sp": "aaaavavavavavava", "g2": 6, "w2": 12, "gp": "vvaa", "c0": 24, "c2": 0}
+
+SLIDE = ("g.c0.a.48.96 g.c0.v.0.48 w.c1i w.c2i u.c1i g.c1.a.0.96 w.c1z u.c2i g.c2.v.0.96 w.c2z "
+         "b.0.0.32.4 b.0.32.64.5 b.0.64.96.6 u.c1z u.c2z w.c3z e.01 e.2 d.1.0.96 s.0.32.4 s.32.64.5 s.64.96.6 w.c4z x.0 u.c3z "
+         "s.96.192 d.2.0.32 s.192.224 t.0 x.1 d.2.32.96 u.c4z e.3 e.3p e.4 e.4n h.0 k.0 s.224.288 d.3.0.64 c.0 s.288.352 t.1 x.2 "
+         "d.3.64.96 h.1 k.1 d.4.0.64 s.352.448 d.4.64.96 t.2 h.2 k.2 s.448.480 c.1 c.2 h.4 x.3 t.3 k.4 h.3 k.3 c.3 c.4 c.p")
+SWAP = ("QT nq.a.32.96 nq.v.0.32 %s H wq ga.a.48.96 ga.v.0.48 wa wz gq.a.48.96 gq.v.0.48 wqq ua gb.a.48.96 gb.v.0.48 wb NX ")
+OPT = {
+    "cuts": ((0, 96, 224, 352, 480), (0, 96, 224, 352, 480)),
+    "plan1": "F.0 P XL F.1 O.0 L F.2 F.3 O.1 Q " + SLIDE,
+    "plan2": SWAP % "pp pu" + "n.0.a n.1.a PVa PVb n.2.a v.0.v PVc n.3.a XN v.1.v m.0.a v.2.v r.0 m.1.a F.0 v.3.v r.1 m.2.a F.1 O.0 "
+             "r.2 m.3.v F.2 r.3 F.3 O.1 U " + SLIDE,
+    "plan3": SWAP % "LM.p" + "n.0.a n.1.a PVb v.0.v v.1.a v.2.v LM.n m.0.v m.1.a LM.v r.0 r.1 S.f LS S.l n.2.a m.2.v r.2 S.n "
+             "v.3.v n.3.a m.3.v r.3",
+    "near": 2, "oq": "s",
+}
+OPT["plan1"] = ("F.0 XL F.1 P g.c0.v.0.48 O.0 g.c0.a.48.96 L w.c1i F.3 F.2 u.c1i g.c1.a.48.96 w.c1z w.c2i u.c1z O.1 d.0.0.48 g.c1.a.0.48 "
+                "d.0.48.96 w.c3z u.c2i d.1.48.96 Q d.1.0.48 s.0.48 w.c2z s.48.96 g.c2.a.48.96 u.c3z x.0 e.2 g.c2.a.0.48 u.c2z e.01 w.c4z "
+                "e.3 s.96.192 h.0 d.2.0.32 e.3p u.c4z s.192.224 x.1 d.2.32.96 b.4.0.32.6 s.224.288 t.0 d.3.0.64 d.4.32.64 d.3.64.96 k.0 "
+                "d.4.64.96 s.288.352 e.4 e.4n s.416.448 s.384.416.6 c.0 x.2 t.1 s.352.384 h.1 h.2 k.1 t.2 s.448.480 k.2 c.1 x.3 c.2 t.3 "
+                "h.3 k.3 h.4 c.3 k.4 c.4 c.p")
+OPT["plan2"] = ("QT H nq.v.0.32 pp nq.a.32.96 pu ga.v.0.48 wq ga.a.48.96 wa gq.v.0.48 gq.a.48.96 ua gb.a.48.96 wqq wz gb.v.0.48 NX n.0.a wb "
+                "n.1.a PVa PVb n.2.a v.0.a PVc m.0.a v.3.v XN v.2.a v.1.v m.1.v m.2.a n.3.v m.3.v r.0 r.1 F.0 F.1 r.3 r.2 F.2 g.c0.v.0.48 "
+                "O.0 F.3 O.1 g.c0.a.48.96 w.c1i w.c1z U u.c1i w.c2i g.c1.v.48.96 g.c1.a.0.48 u.c1z w.c2z u.c2i d.0.0.48 g.c2.a.0.48 "
+                "d.1.48.96 d.0.48.96 d.1.0.48 s.0.48 w.c3z e.3p g.c2.a.48.96 s.48.96 x.0 u.c2z e.2 d.2.0.32 d.2.32.96 s.96.192 w.c4z "
+                "u.c3z t.0 s.192.224 u.c4z e.01 d.3.0.64 h.0 k.0 b.4.0.32.6 d.4.32.64 x.1 s.224.288 e.4n s.288.352 e.4 e.3 d.3.64.96 c.0 "
+                "h.2 s.416.448 t.1 x.2 d.4.64.96 h.1 s.384.416.6 k.1 s.352.384 s.448.480 t.2 k.2 x.3 c.1 c.2 h.4 h.3 t.3 k.3 c.3 k.4 c.4 c.p")
+OPT["plan3"] = ("QT H nq.v.0.32 nq.a.32.96 LM.p ga.a.48.96 ga.v.0.48 wq gq.a.48.96 wa wz gq.v.0.48 ua wqq gb.a.48.96 gb.v.0.48 NX wb n.1.a "
+                "PVb n.0.a v.1.a v.0.v n.2.a LM.n m.0.v r.0 m.1.v r.1 v.2.a LM.v S.f LS n.3.a m.2.v S.l r.2 v.3.a S.n m.3.v r.3")
 
 F, B, I, U = "float32", "bfloat16", "int32", "uint16"
 SCRATCH = {
-    "ZT": ("sbuf", [128, W], B), "NP": ("sbuf", [128, W], B), "QT": ("sbuf", [128, W], B),
-    "ZA": ("sbuf", [128, V], B), "ZN": ("sbuf", [128, V], B),
-    "XI": ("sbuf", [128, V], I), "LI": ("sbuf", [128, 288], I), "TI": ("sbuf", [128, 4], I),
-    "LZ": ("sbuf", [128, 288], F), "LT": ("sbuf", [128, 288], B), "LC": ("sbuf", [128, 288], B),
+    "ZT": ("sbuf", [128, W], B), "ZU": ("sbuf", [128, W], B), "NP": ("sbuf", [128, W], B), "QT": ("sbuf", [128, W], B),
+    "ZA": ("sbuf", [128, V], B), "ZN": ("sbuf", [128, V], B), "ZP": ("sbuf", [128, V], B),
+    "XI": ("sbuf", [128, V], I), "LI": ("sbuf", [128, 192], I), "PI": ("sbuf", [128, 96], I), "PR": ("sbuf", [128, 96], I),
+    "TI": ("sbuf", [128, 4], I), "LT": ("sbuf", [128, 192], B), "LC": ("sbuf", [128, 192], B),
     "XS": ("sbuf", [128, V], B), "LAND": ("sbuf", [128, V], B),
     "SX": ("sbuf", [128, 384], B), "XL": ("sbuf", [128, 4, 4, 24], B),
-    "SP": ("sbuf", [128, 384], B), "PL": ("sbuf", [128, 4, 4, 24], B),
     "XQ": ("sbuf", [128, 4, 4, 24], B), "XN": ("sbuf", [128, 4, 4, 24], B), "DT": ("sbuf", [128, 640], F),
     "R0": ("sbuf", [128, V], B), "R1": ("sbuf", [128, V], B), "R2": ("sbuf", [128, V], B),
     "GN": ("sbuf", [128, V], B), "GP": ("sbuf", [128, V], B),
     "DF": ("sbuf", [128, 5 * V], B), "SQ": ("sbuf", [128, 5 * V], F),
-    "WF": ("sbuf", [128, 96 * 90], F), "WB": ("sbuf", [128, 96 * 40], B), "WU": ("sbuf", [128, 96 * 32], U),
+    "WF": ("sbuf", [128, 96 * 64], F), "WB": ("sbuf", [128, 96 * 40], B), "WU": ("sbuf", [128, 96 * 32], U),
     "COL": ("sbuf", [128, 8], F), "WI": ("sbuf", [128, 4], F),
-    "ZB": ("sbuf", [128, 576], B), "ZF": ("sbuf", [128, 192], F), "ONE": ("sbuf", [128, 144], F), "CM": ("sbuf", [128, 384], B),
-    "MC": ("sbuf", [128, 576], B), "ME": ("sbuf", [128, 512], B), "PT": ("sbuf", [128, 128], B),
-    "DM": ("sbuf", [128, 4 * 224], B), "BM": ("sbuf", [128, 4 * 144], B), "MD": ("sbuf", [128, 144], F),
-    "REP": ("sbuf", [128, 512], B), "DG": ("sbuf", [128, 640], B), "PM": ("sbuf", [128, 256], B),
-    "MQ": ("sbuf", [128, 288], B), "IDF": ("sbuf", [128, 128], F), "VR": ("sbuf", [128, 128], F), "MH": ("sbuf", [128, 768], F),
-    "LS": ("sbuf", [128, 4, 4, 24], U), "LL": ("sbuf", [128, 384], U), "LO": ("sbuf", [128, 384], F),
+    "ZB": ("sbuf", [128, 576], B), "ZF": ("sbuf", [128, 192], F), "ONE": ("sbuf", [128, 8], F),
+    "CM": ("sbuf", [128, 384], B), "CR": ("sbuf", [128, 384], B),
+    "MC": ("sbuf", [128, 576], B), "ME": ("sbuf", [128, 512], B), "PT": ("sbuf", [128, 384], B),
+    "DM": ("sbuf", [128, 3 * 224], B), "BM": ("sbuf", [128, 4 * 144], B), "MD": ("sbuf", [128, 8], F),
+    "DG": ("sbuf", [128, 768], B), "PM": ("sbuf", [128, 256], B),
+    "MQ": ("sbuf", [128, 288], B), "IDF": ("sbuf", [128, 256], F), "VR": ("sbuf", [128, 128], F), "MH": ("sbuf", [128, 768], F),
+    "LS": ("sbuf", [128, 4, 4, 24], F), "LL": ("sbuf", [128, 384], F),
     "ZS": ("sbuf", [128, V], B), "ZL": ("sbuf", [128, V], B), "ZO": ("sbuf", [128, V], F),
 }
 for _i in range(8):
     SCRATCH["P%d" % _i] = ("psum", [128, 512], F)
-NDMA = 52
-SEMAPHORES = ["qg", "qv", "qa", "qt", "sent"] + ["d%d" % i for i in range(NDMA)] + ["arrl", "arrp", "arrm"] + \
-    ["arrx%d" % i for i in range(N)] + ["arrz%d" % i for i in range(N)]
+NDMA = 40
+SEMAPHORES = ["qg", "qv", "qa", "qt", "sent"] + ["d%d" % i for i in range(NDMA)] + ["arrp", "arrl"] + \
+    ["arrx%d" % i for i in range(N)] + ["arrz%d" % i for i in range(N)] + ["arrm%d" % i for i in range(N)]
 
 ADD, SUB, MUL, MIN = AluOpType.add, AluOpType.subtract, AluOpType.mult, AluOpType.min
 EQ, NE, LT, GE = AluOpType.is_equal, AluOpType.not_equal, AluOpType.is_lt, AluOpType.is_ge
-COPY, SQUARE = ActivationFunctionType.Copy, ActivationFunctionType.Square
+COPY, SQUARE, IDENT = ActivationFunctionType.Copy, ActivationFunctionType.Square, ActivationFunctionType.Identity
 
 
 def rank_program(g, core, T, topo):
@@ -63,7 +90,7 @@ def rank_program(g, core, T, topo):
             h = len(off) // len(fr)
             i = fr.index(dst)
             return off[i * h:(i + 1) * h]
-        return [e for e in topo.engines(cs, cores[dst]) if e not in off]
+        return [e for e in topo.engines(cs, cores[dst]) if e not in off][::OPT["near"]]
 
     eng = {"g": g, "v": g.vector, "a": g.scalar, "t": g.tensor, "s": g.sync}
     qsem = {"g": "qg", "v": "qv", "a": "qa", "t": "qt"}
@@ -78,8 +105,8 @@ def rank_program(g, core, T, topo):
         ap = T[name][:, lo:hi] if step == 1 else T[name][:, lo:hi:step]
         return (ap, name, lo, hi, tag)
 
-    def X(ap, name, tag=None):
-        return (ap, name, 0, 1 << 20, tag)
+    def X(ap, name, tag=None, lo=0, hi=1 << 20):
+        return (ap, name, lo, hi, tag)
 
     def blk(name, r, w=384):
         return A(name, w * r, w * r + w)
@@ -95,21 +122,21 @@ def rank_program(g, core, T, topo):
             for (_ap, name, lo, hi, tag) in views:
                 bank = SCRATCH[name][0] == "psum"
                 for (l2, h2, tag2, w2, tok2, q2) in hist.get(name, []):
-                    if bank:
-                        if q2 == q and (q == "t" or not (wr or w2)):
-                            continue
-                    elif not (wr or w2) or l2 >= hi or lo >= h2 or (tag is not None and tag2 is not None and tag != tag2):
+                    if bank and q2 == q == "t":
                         continue
+                    if not (bank and q2 != q):
+                        if not (wr or w2) or l2 >= hi or lo >= h2 or (tag is not None and tag2 is not None and tag != tag2):
+                            continue
                     need[tok2[0]] = max(need.get(tok2[0], 0), tok2[1])
         for s in need:
             wait(q, (s, need[s]))
         for views, wr in ((reads, False), (writes, True)):
             for (_ap, name, lo, hi, tag) in views:
                 h = hist.setdefault(name, [])
-                if wr and tag is None and SCRATCH[name][0] != "psum":
-                    h[:] = [e for e in h if not (lo <= e[0] and e[1] <= hi)]
                 if SCRATCH[name][0] == "psum":
-                    h[:] = [e for e in h if e[5] == q and e[3] and not wr]
+                    h[:] = [e for e in h if e[5] == q and q != "t"]
+                if wr and tag is None:
+                    h[:] = [e for e in h if not (lo <= e[0] and e[1] <= hi)]
                 h.append((lo, hi, tag, wr, tok, q))
 
     def op(q, call, reads, writes):
@@ -119,12 +146,13 @@ def rank_program(g, core, T, topo):
         call().then_inc(T.sem[s], 1)
         count[s] = tok[1]
 
-    def dma(q, out, in_, reads, writes):
+    def dmas(items):
         s = "d%d" % ndma[0]
         ndma[0] += 1
-        order(q, reads, writes, (s, 16))
-        eng[q].dma_start(out, in_).then_inc(T.sem[s], 16)
-        count[s] = 16
+        count[s] = 16 * len(items)
+        for (q, out, in_, reads, writes) in items:
+            order(q, reads, writes, (s, count[s]))
+            eng[q].dma_start(out, in_).then_inc(T.sem[s], 16)
 
     def arrives(view, sem, n):
         count[sem] = n
@@ -157,6 +185,9 @@ def rank_program(g, core, T, topo):
         else:
             op("a", lambda: g.scalar.activation(out[0], in_[0], COPY), [in_], [out])
 
+    def shift(out, in_, add):
+        op("a", lambda: g.scalar.activation(out[0], in_[0], IDENT, bias=add), [in_], [out])
+
     def fill(view, val):
         op("v", lambda: g.vector.memset(view[0], val), [], [view])
 
@@ -169,28 +200,24 @@ def rank_program(g, core, T, topo):
     def iota(out, pattern, base):
         op("g", lambda: g.iota(out[0], pattern, base, 0, allow_small_or_imprecise_dtypes=True), [], [out])
 
-    def gather(q, win, offs, out, lo, hi):
-        o, w, d = A("WU", 96 * offs + lo, 96 * offs + hi), A(win, 0, W), A(out, 16 * lo, 16 * hi)
+    def gather(q, win, offs, out, lo, hi, at=0):
+        o, w, d = A("WU", 96 * offs + lo, 96 * offs + hi), A(win, 0, W), A(out, at + 16 * lo, at + 16 * hi)
         if q == "v":
             op("v", lambda: g.vector.tensor_copy(d[0], w[0].indirect(o[0])), [o, w], [d])
         else:
             op("a", lambda: g.scalar.activation(d[0], w[0].indirect(o[0]), COPY), [o, w], [d])
 
-    def gather2(win, offs, out):
-        gather("a", win, offs, out, 48, 96)
-        gather("v", win, offs, out, 0, 48)
-
     slots = {"WF": [0], "WB": [0], "WU": [0]}
 
-    def new(buf):
-        slots[buf][0] += 1
-        return slots[buf][0] - 1
+    def new(buf, n=1):
+        slots[buf][0] += n
+        return slots[buf][0] - n
 
-    def wf(i):
-        return blk("WF", i, 96)
+    def wf(i, n=1):
+        return A("WF", 96 * i, 96 * (i + n))
 
-    def wb(i):
-        return blk("WB", i, 96)
+    def wb(i, n=1):
+        return A("WB", 96 * i, 96 * (i + n))
 
     def wu(i):
         return blk("WU", i, 96)
@@ -201,11 +228,14 @@ def rank_program(g, core, T, topo):
     def dg(i):
         return blk("DG", i, 128)
 
-    NXZ, NXI, PVZ, PVI = 0, 1, 2, 3
+    NXZ, PVZ, PVI, NXI = 0, 1, 2, 3
+    SIXTEENTH, TIMES384, PLUS, MINUS, CLOSED, CLOSED4 = range(6)
 
-    def wrap(rows, m, bank):
+    def wrap(rows, m, out, less=None):
+        if less is not None:
+            mm(out, blk("IDF", 1, 128), wf(less), True, False)
         for c in range(16):
-            mm(ps(bank), A("BM", 144 * m + 15 - c, 144 * m + 143 - c), A(rows, c, V, 16), c == 0, c == 15)
+            mm(out, A("BM", 144 * m + 15 - c, 144 * m + 143 - c), A(rows, c, V, 16), c == 0 and less is None, c == 15)
 
     def to_u(src, add):
         i = new("WU")
@@ -214,7 +244,7 @@ def rank_program(g, core, T, topo):
 
     def to_f(src):
         i = new("WF")
-        cp("v", wf(i), src)
+        cp("a", wf(i), src)
         return i
 
     def split(v):
@@ -223,406 +253,407 @@ def rank_program(g, core, T, topo):
         tt(wb(c), v, wb(t), SUB)
         return t, c
 
-    def iform_mm(pc, bank):
-        mm(ps(bank), dg(0), wb(pc[0]), True, False)
-        mm(ps(bank), dg(1), wb(pc[1]), False, True)
+    def form(pc, out, w0, w1):
+        mm(out, w0, wb(pc[0]), True, False)
+        mm(out, w1, wb(pc[1]), False, True)
 
     def mc(r, slot):
         return A("MC", 128 * r + 48 - 16 * slot, 128 * r + 176 - 16 * slot)
 
     def flatten(buf, rows, win, step):
-        for k in range(4):
-            dma(OPT["dq"][k], T[win][32 * k:32 * k + 32:step, :], T[buf][0:rows], [A(buf)], [A(win, tag=k)])
+        dmas([("s", T[win][32 * k:32 * k + 32:step, :], T[buf][0:rows], [A(buf)], [A(win, tag=k)]) for k in range(4)])
 
     def table_out(buf, rows, banks):
         for k in (0, 2, 1, 3):
-            b = "P%d" % banks[k // 2]
-            cp("va"[k // 2], X(T[buf][0:rows, :, k, :], buf, tag=k), X(T[b][0:rows, 96 * (k % 2):96 * (k % 2) + 96], b))
+            b, lo = "P%d" % banks[k // 2], 96 * (k % 2)
+            cp("va"[k // 2], X(T[buf][0:rows, :, k, :], buf, tag=k), X(T[b][0:rows, lo:lo + 96], b, None, lo, lo + 96))
 
-    def fsel(base, cond, delta, out=None):
-        a = new("WF")
-        tt(wf(a), delta, cond, MUL)
+    def pick(base, cond, delta, tmp, out=None):
+        tt(tmp, delta, cond, MUL)
+        i = None
         if out is None:
-            b = new("WF")
-            tt(wf(b), base, wf(a), ADD)
-            return b
-        tt(out, base, wf(a), ADD)
-
-    for j, name in enumerate(("nxt", "prv", "ptn")):
-        dma("s", T.LI[:, 96 * j:96 * j + 96], T[name][:], [], [blk("LI", j, 96)])
-    for r in far + near + [me]:
-        dma("a", blk("XI", r)[0], T.x[32 * r:32 * r + 32, :], [], [blk("XI", r)])
-    for k in range(4):
-        dma("s", T.TI[32 * k:32 * k + 32, 0:1], T.th[32 * me:32 * me + 32, :], [], [A("TI", tag=k)])
-    for r in near + far:
-        arrives(blk("LAND", r), "arrx%d" % r, len(mask_for(r, me)))
-        arrives(blk("ZL", r), "arrz%d" % r, len(mask_for(r, me)))
-    nl = sum(len(mask_for(r, me)) for r in near + far)
-    arrives(A("XL", tag="far"), "arrl", nl)
-    arrives(A("PL", tag="far"), "arrp", nl)
-    arrives(A("LL", tag="far"), "arrm", nl)
-
-    def dmaster(m, pieces):
-        v = blk("DM", m, 224)
-        for n, piece in enumerate(pieces):
-            sel(v, v if n else A("ZB", 0, 224), [[-256, 7], [-64, 2], [-1, 16]], NE, 1.0, 768 - 16 * piece)
-
-    def bmaster(m, row, w0, w1):
-        v = blk("BM", m, 144)
-        sel(v, A("ZB", 0, 144), [[-16, 9], [-256, 16]], NE, w0, 3840 - row)
-        sel(v, v, [[-16, 9], [-256, 16]], NE, w1, 3840 - row - 8)
+            i = new("WF")
+            out = wf(i)
+        tt(out, tmp, base, ADD)
+        return i
 
     fill(A("ZB"), 0.0)
+    dmas([("sa"[n % 2], blk("PI", r, 24)[0], T.ptn[32 * r:32 * r + 32, :], [], [blk("PI", r, 24)]) for n, r in enumerate(far + near)])
+    dmas([("as"[j], blk("LI", j, 96)[0], T[name][:], [], [blk("LI", j, 96)]) for j, name in enumerate(("nxt", "prv"))])
+    for n, r in enumerate(far + near + [me]):
+        dmas([("as"[n % 2], blk("XI", r)[0], T.x[32 * r:32 * r + 32, :], [], [blk("XI", r)])])
+    dmas([("s", blk("PR", me, 24)[0], T.ptn[32 * me:32 * me + 32, :], [], [blk("PR", me, 24)])] +
+         [("s", T.TI[32 * k:32 * k + 32, 0:1], T.th[32 * me:32 * me + 32, :], [], [A("TI", tag=k)]) for k in range(4)])
+    nall = sum(len(mask_for(r, me)) for r in near + far)
+    for r in near + far:
+        n = len(mask_for(r, me))
+        arrives(blk("LAND", r), "arrx%d" % r, n)
+        arrives(blk("ZL", r), "arrz%d" % r, n)
+        arrives(blk("LL", r, 96), "arrm%d" % r, n)
+        arrives(blk("PR", r, 24), "arrp", nall)
+    arrives(A("XL", tag="far"), "arrl", nall)
+
+    def dmaster(m, pieces):
+        v = A("DM", 224 * m + 96, 224 * m + 128)
+        for piece in pieces:
+            sel(v, v, [[-64, 2], [-1, 16]], NE, 1.0, -16 * piece)
+
+    def bmaster(m, row, w0, w1):
+        v = A("BM", 144 * m + 15, 144 * m + 144, 16)
+        sel(v, v, [[-16, 9]], NE, w0, -row)
+        sel(v, v, [[-16, 9]], NE, w1, -row - 8)
+
+    def diag(i, w):
+        sel(dg(i), A("ZB", 0, 128), [[-1, 128]], NE, w, 0)
+
     fill(A("NP", 0, 2048), 0.0)
-    for b in range(4):
-        fill(X(T.WI[32 * b:32 * b + 32, 0:1], "WI", tag=b), 384.0 if b % 2 else 1.0 / 16)
+    fill(A("DM"), 0.0)
+    fill(A("BM"), 0.0)
     cp("a", A("NP", 2048, 4096), A("NP", 0, 2048))
     sel(A("MC"), A("ZB"), [[-16, 9], [-256, 4], [-1, 16]], NE, 1.0, 768)
-    dmaster(NXZ, (0, 2))
-    bmaster(NXI, 0, 1.0 / 16, 384.0)
-    sel(A("ME"), A("ZB", 0, 512), [[-1, 4], [0, 4], [-4, 32]], NE, 1.0, 0)
 
-    for lo, hi in ((0, 192), (192, 288)):
-        ts(A("LZ", lo, hi), A("LI", lo, hi), -ZOFF, None, ADD)
-        ts(A("LT", lo, hi), A("LZ", lo, hi), M16, M16, ADD, SUB)
-        tt(A("LC", lo, hi), A("LZ", lo, hi), A("LT", lo, hi), SUB)
+    send([(r, blk("PI", r, 24), blk("PR", me, 24)[0], "arrp") for r in far + near])
+    z = ps(2, 0, 192)
+    ts(z, A("LI"), -ZOFF, None, ADD)
+    ts(A("LT"), z, M16, M16, ADD, SUB)
+    tt(A("LC"), z, A("LT"), SUB)
     for r in range(N):
         for slot, (src, j) in enumerate((("LT", 0), ("LT", 1), ("LC", 0), ("LC", 1))):
             mm(ps(0, 96 * r), mc(r, slot), blk(src, j, 96), slot == 0, slot == 3)
-    for r in range(N):
-        mm(ps(1, 96 * r), mc(r, 0), blk("LT", 2, 96), True, False)
-        mm(ps(1, 96 * r), mc(r, 2), blk("LC", 2, 96), False, True)
     cp("a", A("SX"), ps(0, 0, 384))
-    cp("a", A("SP"), ps(1, 0, 384))
-    cp("a", A("NP", 4096, W), A("NP", 0, 2048))
+    cp("a", X(T.XL[:, me], "XL", tag="own"), ps(0, 96 * me))
+    sel(blk("PT", 0, 128), A("ZB", 0, 128), [[-1, 4], [-4, 32]], NE, 1.0, 0)
     send([(r, blk("SX", r, 96), T.XL[:, me], "arrl") for r in far + near])
-    send([(r, blk("SP", r, 96), T.PL[:, me], "arrp") for r in far + near])
     for r in far + near:
         cp("v", blk("XS", r), blk("XI", r))
     send([(r, blk("XS", r), blk("LAND", me)[0], "arrx%d" % me) for r in far + near])
     cp("v", blk("LAND", me), blk("XI", me))
-    cp("v", X(T.XL[:, me], "XL", tag="own"), blk("SX", me, 96))
-    cp("v", X(T.PL[:, me], "PL", tag="own"), blk("SP", me, 96))
-    flatten("XL", 128, "NP", 4)
+    cp("a", A("NP", 4096, W), A("NP", 0, 2048))
 
     wi = X(T.WI[:, 0:1], "WI")
-    ts(blk("DM", NXI, 224), blk("DM", NXZ, 224), wi[0], None, MUL, extra=[wi])
+    th = A("COL", 2, 3)
+    for b in range(4):
+        fill(X(T.WI[32 * b:32 * b + 32, 0:1], "WI", tag=b), 384.0 if b % 2 else 1.0 / 16)
+    for i, w in ((1, 1.0 / 16), (2, 384.0)):
+        ts(blk("PT", i, 128), blk("PT", 0, 128), w, None, MUL)
     fill(A("ZF"), 0.0)
     fill(A("ONE"), 1.0)
     fill(A("CM"), -1.5)
-    cp("v", A("COL", 2, 3), A("TI", 0, 1))
-    th = A("COL", 2, 3)
-    sel(A("PT"), A("ZB", 0, 128), [[-1, 4], [-4, 32]], NE, 1.0, 0)
-    ts(blk("BM", NXZ, 144), blk("BM", NXI, 144), 0.0, None, NE)
+    fill(A("CR"), 4 * M1)
+    cp("v", th, A("TI", 0, 1))
+    if " f." in OPT["plan1"] + OPT["plan2"]:
+        sel(A("ME"), A("ZB", 0, 512), [[-1, 4], [0, 4], [-4, 32]], NE, 1.0, 0)
+    bmaster(NXI, 0, 1.0 / 16, 384.0)
+    bmaster(PVI, 4, 1.0 / 16, 384.0)
+    bmaster(NXZ, 0, 1.0, 1.0)
+    bmaster(PVZ, 4, 1.0, 1.0)
+    dmaster(NXZ, (0, 2))
     dmaster(PVZ, (1, 3))
     iota(A("VR"), [[384, 4], [0, 2], [1, 16]], 0)
     sel(A("VR"), A("VR"), [[-1, 128]], EQ, 0.0, 0)
-    ident0, ident = new("WF"), new("WF")
-    iota(wf(ident0), [[1536, 4], [16, 24]], 0)
-    bmaster(PVI, 4, 1.0 / 16, 384.0)
-    sel(A("MD"), A("ONE"), [[-16, 9], [256, 16]], GE, 0.0, -3840)
-    sel(A("MD"), A("MD"), [[16, 9], [0, 16]], GE, 0.0, 15, -1)
-    sel(dg(4), A("ZB", 0, 128), [[-1, 128]], NE, BIG, 0)
-    sel(A("IDF"), A("ZF", 0, 128), [[-1, 128]], NE, 1.0, 0)
+    ident0, ident = new("WF", 2), new("WF", 2)
+    iota(wf(ident0, 2), [[0, 2], [1536, 4], [16, 24]], 0)
+    for i, w in ((PLUS, 1.0), (MINUS, -1.0)):
+        diag(i, w)
+    sel(A("MD"), A("ONE"), [[-16, 8]], GE, 0.0, 0)
+    sel(A("MD"), A("MD"), [[16, 8]], GE, 0.0, 15, -1)
+    for i, w in ((CLOSED, BIG), (CLOSED4, 4 * BIG)):
+        diag(i, w)
+    for i, w in enumerate((1.0, -1.0)):
+        sel(blk("IDF", i, 128), A("ZF", 0, 128), [[-1, 128]], NE, w, 0)
     sel(A("MQ"), A("ZB", 0, 288), [[-16, 9], [-256, 2], [-1, 16]], NE, 1.0, 256)
-    for i, w in ((0, 1.0 / 16), (1, 384.0), (2, 0.25), (3, 0.5)):
-        sel(dg(i), A("ZB", 0, 128), [[-1, 128]], NE, w, 0)
-    sel(A("REP"), A("ZB", 0, 512), [[-32, 4], [0, 4], [-1, 32]], NE, 1.0, 0)
+    for i, w in ((SIXTEENTH, 1.0 / 16), (TIMES384, 384.0)):
+        diag(i, w)
     for i, w in enumerate((0.25, 0.5)):
         sel(blk("PM", i, 128), A("ZB", 0, 128), [[-1, 32], [-32, 4]], NE, w, 0)
     for k in range(4):
         sel(blk("MH", k, 192), A("ZF"), [[-256, 6], [-1, 32]], NE, 1.0, 512 - 32 * k)
 
-    rot = [0]
+    st = {"u": {}, "e": {}}
+    free = [4, 5, 6, 7]
+    CAND = (ps(0, 0), ps(0, 96), ps(1, 0), ps(1, 96), ps(0, 192))
+    KEY = (ps(4, 0), ps(4, 96), ps(5, 0), ps(5, 96), ps(4, 192))
+    FLAGS = (("2", "0", "1"), ("0", "1", "3"), ("4", "2", "0"), ("1", "3", "3p"), ("4n", "4", "2"))
+    WRAPS = {"c1z": ("R0", NXZ, CAND[1]), "c1i": ("R0", NXI, ps(2)), "c2i": ("R0", PVI, ps(3)), "c2z": ("R0", PVZ, CAND[2]),
+             "c3z": ("R1", NXZ, CAND[3]), "c4z": ("R2", PVZ, CAND[4])}
 
-    def spread(lhsT, rhs, out, banks, q):
-        b = banks[rot[0] % len(banks)]
-        mm(ps(b, 0, 384), lhsT, rhs, True, True)
-        cp(q, out, ps(b, 0, 384))
-        rot[0] += 1
-
-    def source(r):
-        for a in range(5):
-            spread(blk("ME", a, 128) if a < 4 else A("PT"), blk("LAND", r), blk("ZT", 4 * r + a) if a < 4 else blk("ZA", r),
-                   (3, 4, 5, 6, 7, 2, 0) if r == far[1] else (3, 4, 5, 6, 7), "va"[rot[0] % 2])
-
-    def own_list(m, buf, bank):
+    def own_list(m, buf, out):
         for k in range(4):
-            mm(ps(bank), A("DM", 224 * m + 96 - 32 * k, 224 * m + 224 - 32 * k), X(T[buf][:, :, k, :], buf), k == 0, k == 3)
+            mm(out, A("DM", 224 * m + 96 - 32 * k, 224 * m + 224 - 32 * k), X(T[buf][:, :, k, :], buf), k == 0, k == 3)
 
-    st = {}
+    def spread(lhsT, rhs, out, q):
+        free.append(free.pop(0))
+        mm(ps(free[-1], 0, 384), lhsT, rhs, True, True)
+        cp(q, out, ps(free[-1], 0, 384))
 
-    def equal(a, b):
-        e = new("WB")
-        tt(wb(e), a, wf(b), EQ)
-        return e
+    def tables(w, src, blocks, table, zown):
+        r = blocks[int(w[1])]
+        if w[0] == "F":
+            dmas([("s", T[table][32 * k:32 * k + 32, V * r:V * r + V], blk(src, r)[0], [blk(src, r)],
+                   [X(None, table, k, V * r, V * r + V)]) for k in range(4)])
+        elif w[0] == "O":
+            lo = 768 * (blocks[2 * int(w[1])] // 2)
+            dmas([(OPT["oq"], T[zown][32 * k:32 * k + 32, lo:lo + 768], T[src][k:128:4, lo:lo + 768], [A(src, lo, lo + 768)],
+                   [X(None, zown, k, lo, lo + 768)]) for k in range(4)])
+        elif w[0] == "f":
+            spread(blk("ME", int(w[2]), 128), blk(src, r), blk(table, 4 * r + int(w[2])), w[3])
+        else:
+            spread(blk("PT", 0, 128), blk(src, r), blk(zown, r), w[2])
 
-    KEY = (4, 4, 5, 6, 4)
-    DTB = ("P3", "P1", "P3", "P1", "P3")
+    def step(chain, k, more):
+        least, best, _ = st[chain]
+        lt, m = new("WF"), new("WF")
+        tt(ps(7, 0), CAND[k], wf(best), SUB)
+        tt(wf(lt), KEY[k], wf(least), LT)
+        if more:
+            tt(wf(m), KEY[k], wf(least), MIN)
+        st[chain] = (m, pick(wf(best), wf(lt), ps(7, 0), ps(7, 96), ps(7, 384) if (chain, k) == ("q", 4) else None), k)
 
-    def key(k):
-        return ps(KEY[k], 96 * (k % 2))
+    def slide(w, cuts, table, zown):
+        u, e = st["u"], st["e"]
+        what, arg = w[0], w[1]
+        if what == "w":
+            wrap(*WRAPS[arg])
+        elif what == "u":
+            u[arg] = to_u(WRAPS[arg][2], ZOFF if arg[2] == "z" else IOFF)
+        elif what == "e":
+            if arg == "01":
+                i = new("WB", 2)
+                tt(wb(i, 2), ps(0, 0, 192), wf(ident, 2), EQ)
+                e["0"], e["1"] = i, i + 1
+            else:
+                e[arg] = new("WB")
+                tt(wb(e[arg]), CAND[int(arg[0])], wf({"p": st["pv"], "n": st["nx"]}.get(arg[-1], ident)), EQ)
+        elif what == "g":
+            gather(w[2], "NP", u[arg + "i"], {"c0": "R0", "c1": "R1", "c2": "R2"}[arg], int(w[3]), int(w[4]))
+        elif what == "d":
+            k, lo, hi = int(arg), int(w[2]), int(w[3])
+            i = u["c%dz" % k]
+            o, win = A("WU", 96 * i + lo, 96 * i + hi), A(table, 0, W)
+            d, z = A("DF", V * k + 16 * lo, V * k + 16 * hi), A(zown, 16 * lo, 16 * hi)
+            op("v", lambda: g.vector.tensor_tensor(d[0], win[0].indirect(o[0]), z[0], SUB), [o, win, z], [d])
+        elif what == "b":
+            k, lo, hi, bank = int(arg), int(w[2]), int(w[3]), int(w[4])
+            gather("a", table, u["c%dz" % k], "DF", lo, hi, V * k)
+            mm(ps(bank, 0, 16 * (hi - lo)), dg(MINUS), A(zown, 16 * lo, 16 * hi), True, False)
+            mm(ps(bank, 0, 16 * (hi - lo)), dg(PLUS), A("DF", V * k + 16 * lo, V * k + 16 * hi), False, True)
+        elif what == "s":
+            lo, hi = int(arg), int(w[2])
+            d = ps(int(w[3]), 0, 16 * (hi - lo)) if len(w) > 3 else A("DF", 16 * lo, 16 * hi)
+            s = A("SQ", 16 * lo, 16 * hi)
+            op("a", lambda: g.scalar.activation(s[0], d[0], SQUARE), [d], [s])
+        elif what == "x":
+            j = int(arg)
+            lo, hi, b = cuts[j], cuts[j + 1], "P%d" % (3 - j % 2)
+            for c in range(16):
+                mm(X(T[b][0:hi - lo, c:128:16], b), A("SQ", 16 * lo + c, 16 * hi, 16), A("MD"), True, True)
+        elif what == "t":
+            j = int(arg)
+            m, b = cuts[j + 1] - cuts[j], "P%d" % (3 - j % 2)
+            cp("a", X(T.DT[0:m, 128 * j:128 * j + 128], "DT", None, 128 * j, 128 * j + 128), X(T[b][0:m, 0:128], b))
+        elif what == "h":
+            k = int(arg)
+            for n, f in enumerate(FLAGS[k]):
+                mm(KEY[k], dg(CLOSED4 if k else CLOSED), wb(e[f]), n == 0, False)
+        elif what == "k":
+            k = int(arg)
+            for j in range(len(cuts) - 1):
+                lo, hi, m = max(cuts[j], 96 * k), min(cuts[j + 1], 96 * k + 96), cuts[j + 1] - cuts[j]
+                if lo < hi:
+                    mm(A(KEY[k][1], KEY[k][2] + lo - 96 * k, KEY[k][2] + hi - 96 * k),
+                       X(T.DT[0:m, 128 * j:128 * j + 128], "DT", None, 128 * j, 128 * j + 128),
+                       X(T.IDF[0:m, lo - cuts[j]:hi - cuts[j]], "IDF", None, 0, 128), False, hi == 96 * k + 96)
+        elif arg == "0":
+            st["c"] = (to_f(KEY[0]), st["p"], 0)
+            st["q"] = None
+        elif arg != "p":
+            step(what, int(arg), int(arg) < 4 or st["q"] is None)
+        else:
+            least, best, k = st["c"]
+            ok, mt = new("WF"), new("WF")
+            tt(ps(7, 0), wf(best), wf(ident), SUB)
+            ts(wf(ok), wf(least), th[0], None, LT, extra=[th])
+            if k < 4:
+                ts(wf(mt), wf(least), th[0], None, MIN, extra=[th])
+            st["q"] = (mt, pick(wf(ident), wf(ok), ps(7, 0), ps(7, 96), ps(7, 384) if k == 4 else None), k)
 
-    def diff(k, offs, zown, lo=0, hi=96):
-        o, w = A("WU", 96 * offs + lo, 96 * offs + hi), A("ZT", 0, W)
-        d, z = A("DF", V * k + 16 * lo, V * k + 16 * hi), A(zown, 16 * lo, 16 * hi)
-        op("v", lambda: g.vector.tensor_tensor(d[0], w[0].indirect(o[0]), z[0], SUB), [o, w, z], [d])
+    def begin(w):
+        if w[0] == "P":
+            ts(ps(2), A("PR"), -ZOFF, None, ADD)
+            pc = split(ps(2))
+            form(pc, ps(1), blk("PT", 1, 128), blk("PT", 2, 128))
+            form(pc, CAND[0], blk("PT", 0, 128), blk("PT", 0, 128))
+            st["u"]["c0i"] = to_u(ps(1), IOFF)
+            st["u"]["c0z"] = to_u(CAND[0], ZOFF)
+            st["p"] = to_f(CAND[0])
+        elif w[0] == "XL":
+            flatten("XL", 128, "NP", 4)
+        elif w[0] == "L":
+            ts(A("DM", 224 * PVI + 96, 224 * PVI + 128), A("DM", 224 * PVZ + 96, 224 * PVZ + 128), wi[0], None, MUL, extra=[wi])
+            own_list(NXZ, "XL", ps(3))
+            own_list(PVZ, "XL", ps(3, 96))
+            own_list(PVI, "XL", ps(2))
+            i = new("WF", 2)
+            cp("a", wf(i, 2), ps(3, 0, 192))
+            st["nx"], st["pv"] = i, i + 1
+            v, o = A("VR"), A("COL", 1, 2)
+            op("v", lambda: g.vector.tensor_reduce(o[0], v[0], AxisListType.X, ADD), [v], [o])
+            ts(wf(ident, 2), wf(ident0, 2), T.COL[:, 1:2], -ZOFF, ADD, ADD, extra=[o])
+            st["pvi"] = to_u(ps(2), IOFF)
+        else:
+            dmas([("s", T.QT[:], T.ZT[:], [A("ZT")], [A("QT")])])
 
-    def square(k, lo=0, hi=96):
-        d, s = A("DF", V * k + 16 * lo, V * k + 16 * hi), A("SQ", V * k + 16 * lo, V * k + 16 * hi)
-        op("a", lambda: g.scalar.activation(s[0], d[0], SQUARE), [d], [s])
+    quarter, half = blk("PM", 0, 128), blk("PM", 1, 128)
 
-    def dist(k):
-        for c in range(16):
-            mm(X(T[DTB[k]][0:96, c:128:16], DTB[k]), A("SQ", V * k + c, V * k + V, 16), A("MD", 15, 128, 16), True, True)
-
-    def turn(k, flags):
-        d = (T.DT[0:96, 128 * k:128 * k + 128], "DT", 128 * k, 128 * k + 128, None)
-        cp("a", d, X(T[DTB[k]][0:96, 0:128], DTB[k]))
-        for n, e in enumerate(flags):
-            mm(key(k), dg(4), wb(e), n == 0, False)
-        mm(key(k), d, X(T.IDF[0:96, 0:96], "IDF"), False, True)
-
-    def choose(c, flags):
-        least, best, d, qb, dp, q = new("WF"), ps(7, 0), ps(7, 96), ps(7, 192), ps(7, 288), ps(7, 384)
-        ts(wf(least), key(0), BIG, None, MIN)
-        for k in range(1, 4):
-            lt, m = new("WF"), new("WF")
-            old = best if k > 1 else wf(c[0])
-            tt(wf(lt), key(k), wf(least), LT)
-            tt(d, wf(c[k]), old, SUB)
-            tt(wf(m), key(k), wf(least), MIN)
-            fsel(old, wf(lt), d, best)
-            least = m
-            if k == 1:
-                turn(4, flags)
-        ok, mt, lq, lp = [new("WF") for _ in range(4)]
-        ts(wf(ok), wf(least), th[0], None, LT, extra=[th])
-        tt(d, best, wf(ident), SUB)
-        ts(wf(mt), wf(least), th[0], None, MIN, extra=[th])
-        fsel(wf(ident), wf(ok), d, qb)
-        tt(dp, wf(c[4]), best, SUB)
-        tt(d, wf(c[4]), qb, SUB)
-        tt(wf(lq), key(4), wf(mt), LT)
-        fsel(qb, wf(lq), d, q)
-        return q, (best, least, lp, dp)
-
-    def begin():
-        source(me)
-        v, o = A("VR"), A("COL", 1, 2)
-        op("v", lambda: g.vector.tensor_reduce(o[0], v[0], AxisListType.X, ADD), [v], [o])
-        ts(wf(ident), wf(ident0), T.COL[:, 1:2], -ZOFF, ADD, ADD, extra=[o])
-        ts(blk("DM", PVI, 224), blk("DM", PVZ, 224), wi[0], None, MUL, extra=[wi])
-        own_list(NXZ, "XL", 2)
-        own_list(PVZ, "XL", 1)
-        own_list(PVI, "XL", 0)
-        st["nx"], st["pv"], st["pvi"] = to_f(ps(2)), to_f(ps(1)), to_u(ps(0), IOFF)
-        own_list(NXI, "PL", 0)
-        own_list(NXZ, "PL", 1)
-        pi, st["pz"], st["p"] = to_u(ps(0), IOFF), to_u(ps(1), ZOFF), to_f(ps(1))
-        source(near[0])
-        gather2("NP", pi, "R0")
-        ts(blk("BM", PVZ, 144), blk("BM", PVI, 144), 0.0, None, NE)
-        source(far[0])
-        source(far[1])
-        wrap("R0", NXI, 1)
-        dma("s", T.QT[:], T.ZT[:], [A("ZT")], [A("QT")])
-
-    def slide(zown, cut):
-        wrap("R0", NXZ, 0)
-        wrap("R0", PVI, 2)
-        if cut:
-            diff(0, st["pz"], zown, 0, cut)
-        c1i = to_u(ps(1), IOFF)
-        wrap("R0", PVZ, 1)
-        gather("a", "NP", c1i, "R1", 0, 96)
-        diff(0, st["pz"], zown, cut, 96)
-        square(0)
-        c1z, c2i = to_u(ps(0), ZOFF), to_u(ps(2), IOFF)
-        gather("a", "NP", c2i, "R2", 0, 48)
-        c1 = to_f(ps(0))
-        wrap("R1", NXZ, 0)
-        dist(0)
-        diff(1, c1z, zown)
-        square(1)
-        c2z, c2, e2 = to_u(ps(1), ZOFF), to_f(ps(1)), equal(ps(1), ident)
-        e0, e1 = equal(wf(st["p"]), ident), equal(wf(c1), ident)
-        dist(1)
-        turn(0, (e2, e0, e1))
-        gather("a", "NP", c2i, "R2", 48, 96)
-        wrap("R2", PVZ, 2)
-        diff(2, c2z, zown)
-        square(2)
-        c3z, c3, e3, e3p = to_u(ps(0), ZOFF), to_f(ps(0)), equal(ps(0), ident), equal(ps(0), st["pv"])
-        dist(2)
-        turn(1, (e0, e1, e3))
-        for lo in (0, 48):
-            diff(3, c3z, zown, lo, lo + 48)
-            square(3, lo, lo + 48)
-        c4z, c4, e4, e4n = to_u(ps(2), ZOFF), to_f(ps(2)), equal(ps(2), ident), equal(ps(2), st["nx"])
-        turn(2, (e4, e2, e0))
-        dist(3)
-        for lo in (0, 48):
-            diff(4, c4z, zown, lo, lo + 48)
-            square(4, lo, lo + 48)
-        turn(3, (e1, e3, e3p))
-        dist(4)
-        return [st["p"], c1, c2, c3, c4], (e4n, e4, e2)
-
-    def list_mm(i, row, stop):
-        for k in range(4):
-            o = 192 * k + 64 - 32 * row
-            mm(ps(3, 96 * k), A("MH", o, o + 128), wf(i), False, stop and k == 3)
-
-    def swap_smooth(c, flags, zown, last):
-        blocks = far + near + [me] if last else [0, 1, 2, 3]
-        quarter, half = (blk("PM", 0, 128), blk("PM", 1, 128)) if last else (dg(2), dg(3))
-
-        def term(n, buf, stop):
-            mm(ps(4 + n, 0, 384), quarter, blk(buf, blocks[n]), False, stop)
-
-        def part(qn, offs, buf, n):
-            gather(qn, "ZT", offs, buf, 24 * blocks[n], 24 * blocks[n] + 24)
-
-        def rounded(buf, n):
-            ts(blk(buf, blocks[n]), ps(4 + n, 0, 384), M1, M1, ADD, SUB)
-
-        def np_mm(pc, slot, stop):
-            for k in range(4):
-                for piece in range(2):
-                    mm(ps((1, 3)[k // 2], 96 * (k % 2)), mc(k, slot + 2 * piece), wb(pc[piece]), False, stop and k % 2 == 1 and piece == 1)
-
-        q, pend = choose(c, flags)
-        qp = split(q)
+    def np_mm(pc, slot, stop):
         for k in range(4):
             for piece in range(2):
-                b, o = "P%d" % (k // 2), 64 * k + 16 - 16 * piece
-                mm(X(T[b][0:64, 96 * (k % 2):96 * (k % 2) + 96], b), A("MQ", o, o + 64), wb(qp[piece]), piece == 0, piece == 1)
-        iform_mm(qp, 2)
-        best, least, lp, dp = pend
-        tt(wf(lp), key(4), wf(least), LT)
-        table_out("XQ", 64, (0, 1))
-        flatten("XQ", 64, "QT", 8)
-        qi = to_u(ps(2), IOFF)
-        gather2("NP", qi, "R0")
-        p = fsel(best, wf(lp), dp)
-        for n in range(4):
-            if n == 3:
-                wrap("R0", NXZ, 2)
-            mm(ps(4 + n, 0, 384), half, blk(zown, blocks[n]), True, False)
-            mm(ps(4 + n, 0, 384), quarter, A("CM"), False, False)
-        if not last:
-            pp = split(wf(p))
-            iform_mm(pp, 3)
-        dn, da, sw, sv = [new("WF") for _ in range(4)]
-        gather2("QT", st["pvi"], "R2")
-        wrap("R2", NXI, 0)
-        tt(wf(dn), ps(2), wf(st["nx"]), SUB)
-        gather2("QT", qi, "R1")
-        wrap("R1", NXZ, 1)
-        ai = to_u(ps(0), IOFF)
-        gather2("QT", ai, "R0")
-        wrap("R2", NXZ, 2)
-        wrap("R0", NXZ, 0)
-        tt(wf(sw), ps(1), wf(ident), EQ)
-        nx = fsel(wf(st["nx"]), wf(sw), wf(dn))
-        nz = to_u(wf(nx), ZOFF)
-        for n in range(3 if last else 4):
-            part("a", nz, "GN", n)
-        if last:
-            mm(ps(3, 0, 384), A("ZB", 0, 128), A("ZB", 0, 384), True, False)
-            list_mm(p, 2, False)
-            for n in range(3):
-                term(n, "GN", False)
-        else:
-            st["pi"] = to_u(ps(3), IOFF)
-            npc = split(wf(nx))
-            for b in (1, 3):
+                mm(ps((1, 2)[k // 2], 96 * (k % 2)), mc(k, slot + 2 * piece), wb(pc[piece]), False, stop and k % 2 == 1 and piece == 1)
+
+    def swap(w, table, zown, blocks, outs):
+        what = w[0]
+        if what == "QT":
+            free[:] = []
+            qp = split(ps(7, 384))
+            for k in range(4):
+                for piece in range(2):
+                    b, o, lo = "P%d" % (2 + k // 2), 64 * k + 16 - 16 * piece, 96 * (k % 2)
+                    mm(X(T[b][0:64, lo:lo + 96], b), A("MQ", o, o + 64), wb(qp[piece]), piece == 0, piece == 1)
+            form(qp, ps(1, 192), dg(SIXTEENTH), dg(TIMES384))
+            table_out("XQ", 64, (2, 3))
+            flatten("XQ", 64, "QT", 8)
+            st["qi"] = to_u(ps(1, 192), IOFF)
+        elif what == "nq":
+            gather(w[1], "NP", st["qi"], "R0", int(w[2]), int(w[3]))
+        elif what == "wq":
+            wrap("R0", NXZ, ps(2), st["nx"])
+        elif what == "pp":
+            st["p"] = st["c"][1]
+            st["pp"] = split(wf(st["p"]))
+            form(st["pp"], ps(3, 288), dg(SIXTEENTH), dg(TIMES384))
+            st["u"]["c0z"] = to_u(wf(st["p"]), ZOFF)
+        elif what == "pu":
+            st["u"]["c0i"] = to_u(ps(3, 288), IOFF)
+        elif what == "H":
+            for n in range(4):
+                mm(ps(4 + n, 0, 384), half, blk(zown, blocks[n]), True, False)
+                mm(ps(4 + n, 0, 384), quarter, A("CM"), False, False)
+        elif what == "ga":
+            gather(w[1], "QT", st["pvi"], "R2", int(w[2]), int(w[3]))
+        elif what == "wa":
+            wrap("R2", NXI, ps(0))
+        elif what == "wz":
+            wrap("R2", NXZ, ps(3), st["pv"])
+        elif what == "ua":
+            st["ai"] = to_u(ps(0), IOFF)
+        elif what == "gq":
+            gather(w[1], "QT", st["qi"], "R1", int(w[2]), int(w[3]))
+        elif what == "wqq":
+            wrap("R1", NXZ, ps(2, 288))
+        elif what == "gb":
+            gather(w[1], "QT", st["ai"], "R0", int(w[2]), int(w[3]))
+        elif what == "wb":
+            wrap("R0", NXZ, ps(0))
+        elif what == "NX":
+            sw = new("WF")
+            tt(wf(sw), ps(2, 288), wf(ident), EQ)
+            st["nx"] = pick(wf(st["nx"]), wf(sw), ps(2), ps(2, 192))
+            st["nz"] = to_u(wf(st["nx"]), ZOFF)
+        elif what == "PVa":
+            npc = split(wf(st["nx"]))
+            for b in (1, 2):
                 mm(ps(b, 0, 192), A("ZB", 0, 128), A("ZB", 0, 192), True, False)
             np_mm(npc, 0, False)
-        tt(wf(da), ps(2), wf(st["pv"]), SUB)
-        tt(wf(sv), ps(0), wf(st["pv"]), EQ)
-        pv = fsel(wf(st["pv"]), wf(sv), wf(da))
-        vz = to_u(wf(pv), ZOFF)
-        if last:
-            land = blk("ZL", me)[0]
-            part("v", vz, "GP", 0)
-            part("a", vz, "GP", 1)
-            part("a", vz, "GP", 2)
-            part("a", nz, "GN", 3)
-            part("a", vz, "GP", 3)
-            for n in range(2):
-                term(n, "GP", True)
-                rounded("ZS", n)
-            send([(r, blk("ZS", r), land, "arrz%d" % me) for r in far])
-            list_mm(pv, 1, False)
-            term(2, "GP", True)
-            list_mm(nx, 0, True)
-            term(3, "GN", False)
-            term(3, "GP", True)
-            rounded("ZS", 2)
+        elif what == "PVb":
+            sv = new("WF")
+            tt(wf(sv), ps(0), wf(st["pv"]), EQ)
+            st["pv"] = pick(wf(st["pv"]), wf(sv), ps(3), ps(3, 192))
+            st["vz"] = to_u(wf(st["pv"]), ZOFF)
+        elif what == "PVc":
+            vpc = split(wf(st["pv"]))
+            np_mm(vpc, 1, True)
+            form(vpc, ps(3), dg(SIXTEENTH), dg(TIMES384))
+            form(st["pp"], CAND[0], dg(PLUS), dg(PLUS))
+        elif what == "XN":
+            table_out("XN", 128, (1, 2))
+            flatten("XN", 128, "NP", 4)
+        elif what == "U":
+            st["pvi"] = to_u(ps(3), IOFF)
+        elif what in "nv":
+            n = blocks[int(w[1])]
+            gather(w[2], table, st[what + "z"], {"n": "GN", "v": "GP"}[what], 24 * n, 24 * n + 24)
+        elif what == "m":
+            n = int(w[1])
+            mm(ps(4 + n, 0, 384), quarter, blk("GN", blocks[n]), False, False)
+            mm(ps(4 + n, 0, 384), quarter, blk("GP", blocks[n]), False, w[2] == "v")
+            if w[2] == "a":
+                mm(ps(4 + n, 0, 384), quarter, A("CR"), False, True)
+            st["round", n] = w[2]
+        elif what == "r":
+            n = int(w[1])
+            if st["round", n] == "v":
+                ts(blk(outs[n], blocks[n]), ps(4 + n, 0, 384), M1, M1, ADD, SUB)
+            else:
+                shift(blk(outs[n], blocks[n]), ps(4 + n, 0, 384), -M1)
+            free.insert(0, 4 + n)
+        elif what == "LM":
+            i, row = {"n": (st["nx"], 0), "v": (st["pv"], 1), "p": (st["c"][1], 2)}[w[1]]
+            if w[1] == "p":
+                mm(ps(1, 0, 384), A("ZB", 0, 128), A("ZB", 0, 384), True, False)
             for k in range(4):
-                ts(X(T.LS[:, :, k, :], "LS", tag=k), ps(3, 96 * k), ZOFF, None, ADD)
-            send([(r, blk("ZS", r), land, "arrz%d" % me) for r in near])
-            send([(r, X(T.LS[:, r], "LS"), blk("LL", me, 96)[0], "arrm") for r in far + near])
-            rounded("ZO", 3)
-            return
-        gp = OPT["gp"]
-        banks = (0, 2, 4, 0, 5, 2, 6, 4, 7, 0, 5, 2, 6, 4, 7, 0)
-        rot[0] = 0
+                o = 192 * k + 64 - 32 * row
+                mm(ps(1, 96 * k), A("MH", o, o + 128), wf(i), False, w[1] == "v" and k == 3)
+        elif what == "LS":
+            for k in range(4):
+                shift(X(T.LS[:, :, k, :], "LS", tag=k), ps(1, 96 * k), ZOFF)
+        elif w[1] == "l":
+            send([(r, X(T.LS[:, r], "LS"), blk("LL", me, 96)[0], "arrm%d" % me) for r in far + near])
+        else:
+            send([(r, blk("ZS", r), blk("ZL", me)[0], "arrz%d" % me) for r in (far if w[1] == "f" else near)])
 
-        def spreads(lo, hi):
-            for n in range(lo, hi):
-                spread(blk("REP", n % 4, 128), blk("ZN", n // 4), blk("ZT", n), banks, OPT["sp"][n])
+    for word in OPT["plan1"].split():
+        w = word.split(".")
+        if w[0] in "FOfo":
+            tables(w, "LAND", [me] + near + far, "ZT", "ZA")
+        elif w[0] in ("P", "XL", "L", "Q"):
+            begin(w)
+        else:
+            slide(w, OPT["cuts"][0], "ZT", "ZA")
+    for plan, table, zown, blocks, outs in (("plan2", "ZT", "ZA", [0, 1, 2, 3], ["ZP"] * 4),
+                                            ("plan3", "ZU", "ZN", far + near + [me], ["ZS", "ZS", "ZS", "ZO"])):
+        for word in OPT[plan].split():
+            w = word.split(".")
+            if w[0] in "FOfo":
+                tables(w, "ZP", blocks, "ZU", "ZN")
+            elif w[0] in "wuegdbsxthkcq":
+                slide(w, OPT["cuts"][1], "ZU", "ZN")
+            else:
+                swap(w, table, zown, blocks, outs)
 
-        vpc = split(wf(pv))
-        np_mm(vpc, 1, True)
-        part(gp[0], vz, "GP", 0)
-        table_out("XN", 128, (1, 3))
-        flatten("XN", 128, "NP", 4)
-        for n in range(1, 4):
-            part(gp[n], vz, "GP", n)
-        for n in range(4):
-            term(n, "GN", False)
-        for n in range(2):
-            term(n, "GP", True)
-        iform_mm(vpc, 3)
-        rounded("ZN", 0)
-        spreads(0, 2)
-        for n in range(2, 4):
-            term(n, "GP", True)
-        spreads(2, 4)
-        for n in range(1, 4):
-            rounded("ZN", n)
-        st["nx"], st["pv"], st["p"] = nx, pv, p
-        st["pz"], st["pvi"] = to_u(wf(p), ZOFF), to_u(ps(3), IOFF)
-        spreads(4, OPT["g2"])
-        gather2("NP", st["pi"], "R0")
-        spreads(OPT["g2"], OPT["w2"])
-        wrap("R0", NXI, 1)
-        spreads(OPT["w2"], 16)
-
-    begin()
-    cands, flags = slide("ZA", OPT["c0"])
-    swap_smooth(cands, flags, "ZA", False)
-    cands, flags = slide("ZN", OPT["c2"])
-    swap_smooth(cands, flags, "ZN", True)
-
-    def out_lists(r):
+    def out_lists(r, q):
         for row, name in enumerate(("yn", "yv", "yp")):
-            dma("s", T[name][32 * r:32 * r + 32, :], T.LO[32 * row:32 * row + 32, 96 * r:96 * r + 96], [blk("LO", r, 96)], [])
+            if r == me:
+                src, view = T.LS[32 * row:32 * row + 32, r], A("LS")
+            else:
+                src, view = T.LL[32 * row:32 * row + 32, 96 * r:96 * r + 96], blk("LL", r, 96)
+            stores.append((q, T[name][32 * r:32 * r + 32, :], src, [view], []))
 
-    def out_points(r, qn):
-        dma(qn, T.yx[32 * r:32 * r + 32, :], blk("ZO", r)[0], [blk("ZO", r)], [])
+    def out_points(r, q):
+        stores.append((q, T.yx[32 * r:32 * r + 32, :], blk("ZO", r)[0], [blk("ZO", r)], []))
 
-    out_points(me, "a")
-    cp("v", blk("LO", me, 96), X(T.LS[:, me], "LS"))
-    out_lists(me)
-    for r, qn in ((near[0], "a"), (far[0], "a"), (far[1], "v")):
+    stores = []
+    out_lists(me, "s")
+    out_points(me, "s")
+    out_lists(near[0], "s")
+    dmas(stores)
+    for r, qn in ((far[0], "a"), (far[1], "v"), (near[0], "v")):
         cp(qn, blk("ZO", r), blk("ZL", r))
-        out_points(r, "a" if qn == "a" else "s")
-    for r in near + far:
-        cp("v", blk("LO", r, 96), blk("LL", r, 96))
-        out_lists(r)
+    stores = []
+    out_points(far[0], "a")
+    out_points(far[1], "s")
+    out_points(near[0], "s")
+    out_lists(far[0], "a")
+    out_lists(far[1], "s")
+    dmas(stores)
     for s in count:
         wait("g", (s, count[s]))

from concourse.bass import DstId, RemoteDMATransfer
from concourse.mybir import AluOpType, AxisListType, ActivationFunctionType

N, V, W = 4, 1536, 6144
ZOFF = 3079.5
IOFF = 3072.0
M16 = 1.5 * 2 ** 27
M1 = 1.5 * 2 ** 23
BIG = float(2 ** 20)

SLIDE = ("g.c0.a.48.96 g.c0.v.0.48 w.c1i w.c2i u.c1i g.c1.a.0.96 w.c1z u.c2i g.c2.v.0.96 w.c2z "
         "b.0.0.32.4 b.0.32.64.5 b.0.64.96.6 u.c1z u.c2z w.c3z e.01 e.2 d.1.0.96 s.0.32.4 s.32.64.5 s.64.96.6 w.c4z x.0 u.c3z "
         "s.96.192 d.2.0.32 s.192.224 t.0 x.1 d.2.32.96 u.c4z e.3 e.3p e.4 e.4n h.0 k.0 s.224.288 d.3.0.64 c.0 s.288.352 t.1 x.2 "
         "d.3.64.96 h.1 k.1 d.4.0.64 s.352.448 d.4.64.96 t.2 h.2 k.2 s.448.480 c.1 c.2 h.4 x.3 t.3 k.4 h.3 k.3 c.3 c.4 c.p")
SWAP = ("QT nq.a.32.96 nq.v.0.32 %s H wq ga.a.48.96 ga.v.0.48 wa wz gq.a.48.96 gq.v.0.48 wqq ua gb.a.48.96 gb.v.0.48 wb NX ")
OPT = {
    "cuts": ((0, 96, 224, 352, 480), (0, 96, 224, 352, 480)),
    "plan1": "F.0 P XL F.1 O.0 L F.2 F.3 O.1 Q " + SLIDE,
    "plan2": SWAP % "pp pu" + "n.0.a n.1.a PVa PVb n.2.a v.0.v PVc n.3.a XN v.1.v m.0.a v.2.v r.0 m.1.a F.0 v.3.v r.1 m.2.a F.1 O.0 "
             "r.2 m.3.v F.2 r.3 F.3 O.1 U " + SLIDE,
    "plan3": SWAP % "LM.p" + "n.0.a n.1.a PVb v.0.v v.1.a v.2.v LM.n m.0.v m.1.a LM.v r.0 r.1 S.f LS S.l n.2.a m.2.v r.2 S.n "
             "v.3.v n.3.a m.3.v r.3",
    "near": 2, "oq": "s",
}
OPT["plan1"] = ("F.0 XL F.1 P g.c0.v.0.48 O.0 g.c0.a.48.96 L w.c1i F.3 F.2 u.c1i g.c1.a.48.96 w.c1z w.c2i u.c1z O.1 d.0.0.48 g.c1.a.0.48 "
                "d.0.48.96 w.c3z u.c2i d.1.48.96 Q d.1.0.48 s.0.48 w.c2z s.48.96 g.c2.a.48.96 u.c3z x.0 e.2 g.c2.a.0.48 u.c2z e.01 w.c4z "
                "e.3 s.96.192 h.0 d.2.0.32 e.3p u.c4z s.192.224 x.1 d.2.32.96 b.4.0.32.6 s.224.288 t.0 d.3.0.64 d.4.32.64 d.3.64.96 k.0 "
                "d.4.64.96 s.288.352 e.4 e.4n s.416.448 s.384.416.6 c.0 x.2 t.1 s.352.384 h.1 h.2 k.1 t.2 s.448.480 k.2 c.1 x.3 c.2 t.3 "
                "h.3 k.3 h.4 c.3 k.4 c.4 c.p")
OPT["plan2"] = ("QT H nq.v.0.32 pp nq.a.32.96 pu ga.v.0.48 wq ga.a.48.96 wa gq.v.0.48 gq.a.48.96 ua gb.a.48.96 wqq wz gb.v.0.48 NX n.0.a wb "
                "n.1.a PVa PVb n.2.a v.0.a PVc m.0.a v.3.v XN v.2.a v.1.v m.1.v m.2.a n.3.v m.3.v r.0 r.1 F.0 F.1 r.3 r.2 F.2 g.c0.v.0.48 "
                "O.0 F.3 O.1 g.c0.a.48.96 w.c1i w.c1z U u.c1i w.c2i g.c1.v.48.96 g.c1.a.0.48 u.c1z w.c2z u.c2i d.0.0.48 g.c2.a.0.48 "
                "d.1.48.96 d.0.48.96 d.1.0.48 s.0.48 w.c3z e.3p g.c2.a.48.96 s.48.96 x.0 u.c2z e.2 d.2.0.32 d.2.32.96 s.96.192 w.c4z "
                "u.c3z t.0 s.192.224 u.c4z e.01 d.3.0.64 h.0 k.0 b.4.0.32.6 d.4.32.64 x.1 s.224.288 e.4n s.288.352 e.4 e.3 d.3.64.96 c.0 "
                "h.2 s.416.448 t.1 x.2 d.4.64.96 h.1 s.384.416.6 k.1 s.352.384 s.448.480 t.2 k.2 x.3 c.1 c.2 h.4 h.3 t.3 k.3 c.3 k.4 c.4 c.p")
OPT["plan3"] = ("QT H nq.v.0.32 nq.a.32.96 LM.p ga.a.48.96 ga.v.0.48 wq gq.a.48.96 wa wz gq.v.0.48 ua wqq gb.a.48.96 gb.v.0.48 NX wb n.1.a "
                "PVb n.0.a v.1.a v.0.v n.2.a LM.n m.0.v r.0 m.1.v r.1 v.2.a LM.v S.f LS n.3.a m.2.v S.l r.2 v.3.a S.n m.3.v r.3")

F, B, I, U = "float32", "bfloat16", "int32", "uint16"
SCRATCH = {
    "ZT": ("sbuf", [128, W], B), "ZU": ("sbuf", [128, W], B), "NP": ("sbuf", [128, W], B), "QT": ("sbuf", [128, W], B),
    "ZA": ("sbuf", [128, V], B), "ZN": ("sbuf", [128, V], B), "ZP": ("sbuf", [128, V], B),
    "XI": ("sbuf", [128, V], I), "LI": ("sbuf", [128, 192], I), "PI": ("sbuf", [128, 96], I), "PR": ("sbuf", [128, 96], I),
    "TI": ("sbuf", [128, 4], I), "LT": ("sbuf", [128, 192], B), "LC": ("sbuf", [128, 192], B),
    "XS": ("sbuf", [128, V], B), "LAND": ("sbuf", [128, V], B),
    "SX": ("sbuf", [128, 384], B), "XL": ("sbuf", [128, 4, 4, 24], B),
    "XQ": ("sbuf", [128, 4, 4, 24], B), "XN": ("sbuf", [128, 4, 4, 24], B), "DT": ("sbuf", [128, 640], F),
    "R0": ("sbuf", [128, V], B), "R1": ("sbuf", [128, V], B), "R2": ("sbuf", [128, V], B),
    "GN": ("sbuf", [128, V], B), "GP": ("sbuf", [128, V], B),
    "DF": ("sbuf", [128, 5 * V], B), "SQ": ("sbuf", [128, 5 * V], F),
    "WF": ("sbuf", [128, 96 * 64], F), "WB": ("sbuf", [128, 96 * 40], B), "WU": ("sbuf", [128, 96 * 32], U),
    "COL": ("sbuf", [128, 8], F), "WI": ("sbuf", [128, 4], F),
    "ZB": ("sbuf", [128, 576], B), "ZF": ("sbuf", [128, 192], F), "ONE": ("sbuf", [128, 8], F),
    "CM": ("sbuf", [128, 384], B), "CR": ("sbuf", [128, 384], B),
    "MC": ("sbuf", [128, 576], B), "ME": ("sbuf", [128, 512], B), "PT": ("sbuf", [128, 384], B),
    "DM": ("sbuf", [128, 3 * 224], B), "BM": ("sbuf", [128, 4 * 144], B), "MD": ("sbuf", [128, 8], F),
    "DG": ("sbuf", [128, 768], B), "PM": ("sbuf", [128, 256], B),
    "MQ": ("sbuf", [128, 288], B), "IDF": ("sbuf", [128, 256], F), "VR": ("sbuf", [128, 128], F), "MH": ("sbuf", [128, 768], F),
    "LS": ("sbuf", [128, 4, 4, 24], F), "LL": ("sbuf", [128, 384], F),
    "ZS": ("sbuf", [128, V], B), "ZL": ("sbuf", [128, V], B), "ZO": ("sbuf", [128, V], F),
}
for _i in range(8):
    SCRATCH["P%d" % _i] = ("psum", [128, 512], F)
NDMA = 40
SEMAPHORES = ["qg", "qv", "qa", "qt", "sent"] + ["d%d" % i for i in range(NDMA)] + ["arrp", "arrl"] + \
    ["arrx%d" % i for i in range(N)] + ["arrz%d" % i for i in range(N)] + ["arrm%d" % i for i in range(N)]

ADD, SUB, MUL, MIN = AluOpType.add, AluOpType.subtract, AluOpType.mult, AluOpType.min
EQ, NE, LT, GE = AluOpType.is_equal, AluOpType.not_equal, AluOpType.is_lt, AluOpType.is_ge
COPY, SQUARE, IDENT = ActivationFunctionType.Copy, ActivationFunctionType.Square, ActivationFunctionType.Identity


def rank_program(g, core, T, topo):
    me = T.rank_of(core)
    if me is None:
        return
    cores = T.cores
    near = [r for r in range(N) if r != me and cores[r] in topo.cores_of(core)]
    far = [r for r in range(N) if r != me and r not in near]
    far.sort(key=lambda r: topo.die(cores[r]) != topo.die(core))

    def bits(es):
        return sum(1 << e for e in es)

    def mask_for(src, dst):
        cs = cores[src]
        fr = [r for r in range(N) if r != src and cores[r] not in topo.cores_of(cs)]
        off = topo.engines(cs, cores[fr[0]])
        if dst in fr:
            h = len(off) // len(fr)
            i = fr.index(dst)
            return off[i * h:(i + 1) * h]
        return [e for e in topo.engines(cs, cores[dst]) if e not in off][::OPT["near"]]

    eng = {"g": g, "v": g.vector, "a": g.scalar, "t": g.tensor, "s": g.sync}
    qsem = {"g": "qg", "v": "qv", "a": "qa", "t": "qt"}
    count = {}
    seen = {q: {} for q in eng}
    hist = {}
    ndma = [0]

    def A(name, lo=None, hi=None, step=1, tag=None):
        if lo is None:
            return (T[name][:], name, 0, 1 << 20, tag)
        ap = T[name][:, lo:hi] if step == 1 else T[name][:, lo:hi:step]
        return (ap, name, lo, hi, tag)

    def X(ap, name, tag=None, lo=0, hi=1 << 20):
        return (ap, name, lo, hi, tag)

    def blk(name, r, w=384):
        return A(name, w * r, w * r + w)

    def wait(q, tok):
        if seen[q].get(tok[0], 0) < tok[1]:
            eng[q].wait_ge(T.sem[tok[0]], tok[1])
            seen[q][tok[0]] = tok[1]

    def order(q, reads, writes, tok):
        need = {}
        for views, wr in ((reads, False), (writes, True)):
            for (_ap, name, lo, hi, tag) in views:
                bank = SCRATCH[name][0] == "psum"
                for (l2, h2, tag2, w2, tok2, q2) in hist.get(name, []):
                    if bank and q2 == q == "t":
                        continue
                    if not (bank and q2 != q):
                        if not (wr or w2) or l2 >= hi or lo >= h2 or (tag is not None and tag2 is not None and tag != tag2):
                            continue
                    need[tok2[0]] = max(need.get(tok2[0], 0), tok2[1])
        for s in need:
            wait(q, (s, need[s]))
        for views, wr in ((reads, False), (writes, True)):
            for (_ap, name, lo, hi, tag) in views:
                h = hist.setdefault(name, [])
                if SCRATCH[name][0] == "psum":
                    h[:] = [e for e in h if e[5] == q and q != "t"]
                if wr and tag is None:
                    h[:] = [e for e in h if not (lo <= e[0] and e[1] <= hi)]
                h.append((lo, hi, tag, wr, tok, q))

    def op(q, call, reads, writes):
        s = qsem[q]
        tok = (s, count.get(s, 0) + 1)
        order(q, reads, writes, tok)
        call().then_inc(T.sem[s], 1)
        count[s] = tok[1]

    def dmas(items):
        s = "d%d" % ndma[0]
        ndma[0] += 1
        count[s] = 16 * len(items)
        for (q, out, in_, reads, writes) in items:
            order(q, reads, writes, (s, count[s]))
            eng[q].dma_start(out, in_).then_inc(T.sem[s], 16)

    def arrives(view, sem, n):
        count[sem] = n
        hist.setdefault(view[1], []).append((view[2], view[3], view[4], True, (sem, n), "r"))

    def send(items):
        trs, n = [], 0
        for (r, src, dst, sem) in items:
            rid, pid = topo.addr(cores[r], core)
            es = mask_for(me, r)
            n += len(es)
            trs.append(RemoteDMATransfer(dst_ids=[DstId(rid=rid, pnc=pid)], dma_engine_mask=bits(es), remote_sem=T.sem[sem],
                                         src=src[0], dst=dst))
        order("g", [it[1] for it in items], [], ("sent", 1 << 20))
        g.remote_dma_fused(trs, local_sem=T.sem.sent)
        count["sent"] = count.get("sent", 0) + n

    def ts(out, in0, s1, s2, o0, o1=None, extra=()):
        if o1 is None:
            op("v", lambda: g.vector.tensor_scalar(out[0], in0[0], s1, None, o0), [in0] + list(extra), [out])
        else:
            op("v", lambda: g.vector.tensor_scalar(out[0], in0[0], s1, s2, o0, o1), [in0] + list(extra), [out])

    def tt(out, a, b, o):
        op("v", lambda: g.vector.tensor_tensor(out[0], a[0], b[0], o), [a, b], [out])

    def cp(q, out, in_):
        if q == "v":
            op("v", lambda: g.vector.tensor_copy(out[0], in_[0]), [in_], [out])
        else:
            op("a", lambda: g.scalar.activation(out[0], in_[0], COPY), [in_], [out])

    def shift(out, in_, add):
        op("a", lambda: g.scalar.activation(out[0], in_[0], IDENT, bias=add), [in_], [out])

    def fill(view, val):
        op("v", lambda: g.vector.memset(view[0], val), [], [view])

    def mm(out, lhsT, rhs, start, stop):
        op("t", lambda: g.tensor.matmul(out[0], lhsT[0], rhs[0], start, stop), [lhsT, rhs], [out])

    def sel(out, in_, pattern, cmp, val, base, cm=1):
        op("g", lambda: g.affine_select(out[0], in_[0], pattern, cmp, val, base, cm), [in_], [out])

    def iota(out, pattern, base):
        op("g", lambda: g.iota(out[0], pattern, base, 0, allow_small_or_imprecise_dtypes=True), [], [out])

    def gather(q, win, offs, out, lo, hi, at=0):
        o, w, d = A("WU", 96 * offs + lo, 96 * offs + hi), A(win, 0, W), A(out, at + 16 * lo, at + 16 * hi)
        if q == "v":
            op("v", lambda: g.vector.tensor_copy(d[0], w[0].indirect(o[0])), [o, w], [d])
        else:
            op("a", lambda: g.scalar.activation(d[0], w[0].indirect(o[0]), COPY), [o, w], [d])

    slots = {"WF": [0], "WB": [0], "WU": [0]}

    def new(buf, n=1):
        slots[buf][0] += n
        return slots[buf][0] - n

    def wf(i, n=1):
        return A("WF", 96 * i, 96 * (i + n))

    def wb(i, n=1):
        return A("WB", 96 * i, 96 * (i + n))

    def wu(i):
        return blk("WU", i, 96)

    def ps(b, lo=0, n=96):
        return A("P%d" % b, lo, lo + n)

    def dg(i):
        return blk("DG", i, 128)

    NXZ, PVZ, PVI, NXI = 0, 1, 2, 3
    SIXTEENTH, TIMES384, PLUS, MINUS, CLOSED, CLOSED4 = range(6)

    def wrap(rows, m, out, less=None):
        if less is not None:
            mm(out, blk("IDF", 1, 128), wf(less), True, False)
        for c in range(16):
            mm(out, A("BM", 144 * m + 15 - c, 144 * m + 143 - c), A(rows, c, V, 16), c == 0 and less is None, c == 15)

    def to_u(src, add):
        i = new("WU")
        ts(wu(i), src, add, None, ADD)
        return i

    def to_f(src):
        i = new("WF")
        cp("a", wf(i), src)
        return i

    def split(v):
        t, c = new("WB"), new("WB")
        ts(wb(t), v, M16, M16, ADD, SUB)
        tt(wb(c), v, wb(t), SUB)
        return t, c

    def form(pc, out, w0, w1):
        mm(out, w0, wb(pc[0]), True, False)
        mm(out, w1, wb(pc[1]), False, True)

    def mc(r, slot):
        return A("MC", 128 * r + 48 - 16 * slot, 128 * r + 176 - 16 * slot)

    def flatten(buf, rows, win, step):
        dmas([("s", T[win][32 * k:32 * k + 32:step, :], T[buf][0:rows], [A(buf)], [A(win, tag=k)]) for k in range(4)])

    def table_out(buf, rows, banks):
        for k in (0, 2, 1, 3):
            b, lo = "P%d" % banks[k // 2], 96 * (k % 2)
            cp("va"[k // 2], X(T[buf][0:rows, :, k, :], buf, tag=k), X(T[b][0:rows, lo:lo + 96], b, None, lo, lo + 96))

    def pick(base, cond, delta, tmp, out=None):
        tt(tmp, delta, cond, MUL)
        i = None
        if out is None:
            i = new("WF")
            out = wf(i)
        tt(out, tmp, base, ADD)
        return i

    fill(A("ZB"), 0.0)
    dmas([("sa"[n % 2], blk("PI", r, 24)[0], T.ptn[32 * r:32 * r + 32, :], [], [blk("PI", r, 24)]) for n, r in enumerate(far + near)])
    dmas([("as"[j], blk("LI", j, 96)[0], T[name][:], [], [blk("LI", j, 96)]) for j, name in enumerate(("nxt", "prv"))])
    for n, r in enumerate(far + near + [me]):
        dmas([("as"[n % 2], blk("XI", r)[0], T.x[32 * r:32 * r + 32, :], [], [blk("XI", r)])])
    dmas([("s", blk("PR", me, 24)[0], T.ptn[32 * me:32 * me + 32, :], [], [blk("PR", me, 24)])] +
         [("s", T.TI[32 * k:32 * k + 32, 0:1], T.th[32 * me:32 * me + 32, :], [], [A("TI", tag=k)]) for k in range(4)])
    nall = sum(len(mask_for(r, me)) for r in near + far)
    for r in near + far:
        n = len(mask_for(r, me))
        arrives(blk("LAND", r), "arrx%d" % r, n)
        arrives(blk("ZL", r), "arrz%d" % r, n)
        arrives(blk("LL", r, 96), "arrm%d" % r, n)
        arrives(blk("PR", r, 24), "arrp", nall)
    arrives(A("XL", tag="far"), "arrl", nall)

    def dmaster(m, pieces):
        v = A("DM", 224 * m + 96, 224 * m + 128)
        for piece in pieces:
            sel(v, v, [[-64, 2], [-1, 16]], NE, 1.0, -16 * piece)

    def bmaster(m, row, w0, w1):
        v = A("BM", 144 * m + 15, 144 * m + 144, 16)
        sel(v, v, [[-16, 9]], NE, w0, -row)
        sel(v, v, [[-16, 9]], NE, w1, -row - 8)

    def diag(i, w):
        sel(dg(i), A("ZB", 0, 128), [[-1, 128]], NE, w, 0)

    fill(A("NP", 0, 2048), 0.0)
    fill(A("DM"), 0.0)
    fill(A("BM"), 0.0)
    cp("a", A("NP", 2048, 4096), A("NP", 0, 2048))
    sel(A("MC"), A("ZB"), [[-16, 9], [-256, 4], [-1, 16]], NE, 1.0, 768)

    send([(r, blk("PI", r, 24), blk("PR", me, 24)[0], "arrp") for r in far + near])
    z = ps(2, 0, 192)
    ts(z, A("LI"), -ZOFF, None, ADD)
    ts(A("LT"), z, M16, M16, ADD, SUB)
    tt(A("LC"), z, A("LT"), SUB)
    for r in range(N):
        for slot, (src, j) in enumerate((("LT", 0), ("LT", 1), ("LC", 0), ("LC", 1))):
            mm(ps(0, 96 * r), mc(r, slot), blk(src, j, 96), slot == 0, slot == 3)
    cp("a", A("SX"), ps(0, 0, 384))
    cp("a", X(T.XL[:, me], "XL", tag="own"), ps(0, 96 * me))
    sel(blk("PT", 0, 128), A("ZB", 0, 128), [[-1, 4], [-4, 32]], NE, 1.0, 0)
    send([(r, blk("SX", r, 96), T.XL[:, me], "arrl") for r in far + near])
    for r in far + near:
        cp("v", blk("XS", r), blk("XI", r))
    send([(r, blk("XS", r), blk("LAND", me)[0], "arrx%d" % me) for r in far + near])
    cp("v", blk("LAND", me), blk("XI", me))
    cp("a", A("NP", 4096, W), A("NP", 0, 2048))

    wi = X(T.WI[:, 0:1], "WI")
    th = A("COL", 2, 3)
    for b in range(4):
        fill(X(T.WI[32 * b:32 * b + 32, 0:1], "WI", tag=b), 384.0 if b % 2 else 1.0 / 16)
    for i, w in ((1, 1.0 / 16), (2, 384.0)):
        ts(blk("PT", i, 128), blk("PT", 0, 128), w, None, MUL)
    fill(A("ZF"), 0.0)
    fill(A("ONE"), 1.0)
    fill(A("CM"), -1.5)
    fill(A("CR"), 4 * M1)
    cp("v", th, A("TI", 0, 1))
    if " f." in OPT["plan1"] + OPT["plan2"]:
        sel(A("ME"), A("ZB", 0, 512), [[-1, 4], [0, 4], [-4, 32]], NE, 1.0, 0)
    bmaster(NXI, 0, 1.0 / 16, 384.0)
    bmaster(PVI, 4, 1.0 / 16, 384.0)
    bmaster(NXZ, 0, 1.0, 1.0)
    bmaster(PVZ, 4, 1.0, 1.0)
    dmaster(NXZ, (0, 2))
    dmaster(PVZ, (1, 3))
    iota(A("VR"), [[384, 4], [0, 2], [1, 16]], 0)
    sel(A("VR"), A("VR"), [[-1, 128]], EQ, 0.0, 0)
    ident0, ident = new("WF", 2), new("WF", 2)
    iota(wf(ident0, 2), [[0, 2], [1536, 4], [16, 24]], 0)
    for i, w in ((PLUS, 1.0), (MINUS, -1.0)):
        diag(i, w)
    sel(A("MD"), A("ONE"), [[-16, 8]], GE, 0.0, 0)
    sel(A("MD"), A("MD"), [[16, 8]], GE, 0.0, 15, -1)
    for i, w in ((CLOSED, BIG), (CLOSED4, 4 * BIG)):
        diag(i, w)
    for i, w in enumerate((1.0, -1.0)):
        sel(blk("IDF", i, 128), A("ZF", 0, 128), [[-1, 128]], NE, w, 0)
    sel(A("MQ"), A("ZB", 0, 288), [[-16, 9], [-256, 2], [-1, 16]], NE, 1.0, 256)
    for i, w in ((SIXTEENTH, 1.0 / 16), (TIMES384, 384.0)):
        diag(i, w)
    for i, w in enumerate((0.25, 0.5)):
        sel(blk("PM", i, 128), A("ZB", 0, 128), [[-1, 32], [-32, 4]], NE, w, 0)
    for k in range(4):
        sel(blk("MH", k, 192), A("ZF"), [[-256, 6], [-1, 32]], NE, 1.0, 512 - 32 * k)

    st = {"u": {}, "e": {}}
    free = [4, 5, 6, 7]
    CAND = (ps(0, 0), ps(0, 96), ps(1, 0), ps(1, 96), ps(0, 192))
    KEY = (ps(4, 0), ps(4, 96), ps(5, 0), ps(5, 96), ps(4, 192))
    FLAGS = (("2", "0", "1"), ("0", "1", "3"), ("4", "2", "0"), ("1", "3", "3p"), ("4n", "4", "2"))
    WRAPS = {"c1z": ("R0", NXZ, CAND[1]), "c1i": ("R0", NXI, ps(2)), "c2i": ("R0", PVI, ps(3)), "c2z": ("R0", PVZ, CAND[2]),
             "c3z": ("R1", NXZ, CAND[3]), "c4z": ("R2", PVZ, CAND[4])}

    def own_list(m, buf, out):
        for k in range(4):
            mm(out, A("DM", 224 * m + 96 - 32 * k, 224 * m + 224 - 32 * k), X(T[buf][:, :, k, :], buf), k == 0, k == 3)

    def spread(lhsT, rhs, out, q):
        free.append(free.pop(0))
        mm(ps(free[-1], 0, 384), lhsT, rhs, True, True)
        cp(q, out, ps(free[-1], 0, 384))

    def tables(w, src, blocks, table, zown):
        r = blocks[int(w[1])]
        if w[0] == "F":
            dmas([("s", T[table][32 * k:32 * k + 32, V * r:V * r + V], blk(src, r)[0], [blk(src, r)],
                   [X(None, table, k, V * r, V * r + V)]) for k in range(4)])
        elif w[0] == "O":
            lo = 768 * (blocks[2 * int(w[1])] // 2)
            dmas([(OPT["oq"], T[zown][32 * k:32 * k + 32, lo:lo + 768], T[src][k:128:4, lo:lo + 768], [A(src, lo, lo + 768)],
                   [X(None, zown, k, lo, lo + 768)]) for k in range(4)])
        elif w[0] == "f":
            spread(blk("ME", int(w[2]), 128), blk(src, r), blk(table, 4 * r + int(w[2])), w[3])
        else:
            spread(blk("PT", 0, 128), blk(src, r), blk(zown, r), w[2])

    def step(chain, k, more):
        least, best, _ = st[chain]
        lt, m = new("WF"), new("WF")
        tt(ps(7, 0), CAND[k], wf(best), SUB)
        tt(wf(lt), KEY[k], wf(least), LT)
        if more:
            tt(wf(m), KEY[k], wf(least), MIN)
        st[chain] = (m, pick(wf(best), wf(lt), ps(7, 0), ps(7, 96), ps(7, 384) if (chain, k) == ("q", 4) else None), k)

    def slide(w, cuts, table, zown):
        u, e = st["u"], st["e"]
        what, arg = w[0], w[1]
        if what == "w":
            wrap(*WRAPS[arg])
        elif what == "u":
            u[arg] = to_u(WRAPS[arg][2], ZOFF if arg[2] == "z" else IOFF)
        elif what == "e":
            if arg == "01":
                i = new("WB", 2)
                tt(wb(i, 2), ps(0, 0, 192), wf(ident, 2), EQ)
                e["0"], e["1"] = i, i + 1
            else:
                e[arg] = new("WB")
                tt(wb(e[arg]), CAND[int(arg[0])], wf({"p": st["pv"], "n": st["nx"]}.get(arg[-1], ident)), EQ)
        elif what == "g":
            gather(w[2], "NP", u[arg + "i"], {"c0": "R0", "c1": "R1", "c2": "R2"}[arg], int(w[3]), int(w[4]))
        elif what == "d":
            k, lo, hi = int(arg), int(w[2]), int(w[3])
            i = u["c%dz" % k]
            o, win = A("WU", 96 * i + lo, 96 * i + hi), A(table, 0, W)
            d, z = A("DF", V * k + 16 * lo, V * k + 16 * hi), A(zown, 16 * lo, 16 * hi)
            op("v", lambda: g.vector.tensor_tensor(d[0], win[0].indirect(o[0]), z[0], SUB), [o, win, z], [d])
        elif what == "b":
            k, lo, hi, bank = int(arg), int(w[2]), int(w[3]), int(w[4])
            gather("a", table, u["c%dz" % k], "DF", lo, hi, V * k)
            mm(ps(bank, 0, 16 * (hi - lo)), dg(MINUS), A(zown, 16 * lo, 16 * hi), True, False)
            mm(ps(bank, 0, 16 * (hi - lo)), dg(PLUS), A("DF", V * k + 16 * lo, V * k + 16 * hi), False, True)
        elif what == "s":
            lo, hi = int(arg), int(w[2])
            d = ps(int(w[3]), 0, 16 * (hi - lo)) if len(w) > 3 else A("DF", 16 * lo, 16 * hi)
            s = A("SQ", 16 * lo, 16 * hi)
            op("a", lambda: g.scalar.activation(s[0], d[0], SQUARE), [d], [s])
        elif what == "x":
            j = int(arg)
            lo, hi, b = cuts[j], cuts[j + 1], "P%d" % (3 - j % 2)
            for c in range(16):
                mm(X(T[b][0:hi - lo, c:128:16], b), A("SQ", 16 * lo + c, 16 * hi, 16), A("MD"), True, True)
        elif what == "t":
            j = int(arg)
            m, b = cuts[j + 1] - cuts[j], "P%d" % (3 - j % 2)
            cp("a", X(T.DT[0:m, 128 * j:128 * j + 128], "DT", None, 128 * j, 128 * j + 128), X(T[b][0:m, 0:128], b))
        elif what == "h":
            k = int(arg)
            for n, f in enumerate(FLAGS[k]):
                mm(KEY[k], dg(CLOSED4 if k else CLOSED), wb(e[f]), n == 0, False)
        elif what == "k":
            k = int(arg)
            for j in range(len(cuts) - 1):
                lo, hi, m = max(cuts[j], 96 * k), min(cuts[j + 1], 96 * k + 96), cuts[j + 1] - cuts[j]
                if lo < hi:
                    mm(A(KEY[k][1], KEY[k][2] + lo - 96 * k, KEY[k][2] + hi - 96 * k),
                       X(T.DT[0:m, 128 * j:128 * j + 128], "DT", None, 128 * j, 128 * j + 128),
                       X(T.IDF[0:m, lo - cuts[j]:hi - cuts[j]], "IDF", None, 0, 128), False, hi == 96 * k + 96)
        elif arg == "0":
            st["c"] = (to_f(KEY[0]), st["p"], 0)
            st["q"] = None
        elif arg != "p":
            step(what, int(arg), int(arg) < 4 or st["q"] is None)
        else:
            least, best, k = st["c"]
            ok, mt = new("WF"), new("WF")
            tt(ps(7, 0), wf(best), wf(ident), SUB)
            ts(wf(ok), wf(least), th[0], None, LT, extra=[th])
            if k < 4:
                ts(wf(mt), wf(least), th[0], None, MIN, extra=[th])
            st["q"] = (mt, pick(wf(ident), wf(ok), ps(7, 0), ps(7, 96), ps(7, 384) if k == 4 else None), k)

    def begin(w):
        if w[0] == "P":
            ts(ps(2), A("PR"), -ZOFF, None, ADD)
            pc = split(ps(2))
            form(pc, ps(1), blk("PT", 1, 128), blk("PT", 2, 128))
            form(pc, CAND[0], blk("PT", 0, 128), blk("PT", 0, 128))
            st["u"]["c0i"] = to_u(ps(1), IOFF)
            st["u"]["c0z"] = to_u(CAND[0], ZOFF)
            st["p"] = to_f(CAND[0])
        elif w[0] == "XL":
            flatten("XL", 128, "NP", 4)
        elif w[0] == "L":
            ts(A("DM", 224 * PVI + 96, 224 * PVI + 128), A("DM", 224 * PVZ + 96, 224 * PVZ + 128), wi[0], None, MUL, extra=[wi])
            own_list(NXZ, "XL", ps(3))
            own_list(PVZ, "XL", ps(3, 96))
            own_list(PVI, "XL", ps(2))
            i = new("WF", 2)
            cp("a", wf(i, 2), ps(3, 0, 192))
            st["nx"], st["pv"] = i, i + 1
            v, o = A("VR"), A("COL", 1, 2)
            op("v", lambda: g.vector.tensor_reduce(o[0], v[0], AxisListType.X, ADD), [v], [o])
            ts(wf(ident, 2), wf(ident0, 2), T.COL[:, 1:2], -ZOFF, ADD, ADD, extra=[o])
            st["pvi"] = to_u(ps(2), IOFF)
        else:
            dmas([("s", T.QT[:], T.ZT[:], [A("ZT")], [A("QT")])])

    quarter, half = blk("PM", 0, 128), blk("PM", 1, 128)

    def np_mm(pc, slot, stop):
        for k in range(4):
            for piece in range(2):
                mm(ps((1, 2)[k // 2], 96 * (k % 2)), mc(k, slot + 2 * piece), wb(pc[piece]), False, stop and k % 2 == 1 and piece == 1)

    def swap(w, table, zown, blocks, outs):
        what = w[0]
        if what == "QT":
            free[:] = []
            qp = split(ps(7, 384))
            for k in range(4):
                for piece in range(2):
                    b, o, lo = "P%d" % (2 + k // 2), 64 * k + 16 - 16 * piece, 96 * (k % 2)
                    mm(X(T[b][0:64, lo:lo + 96], b), A("MQ", o, o + 64), wb(qp[piece]), piece == 0, piece == 1)
            form(qp, ps(1, 192), dg(SIXTEENTH), dg(TIMES384))
            table_out("XQ", 64, (2, 3))
            flatten("XQ", 64, "QT", 8)
            st["qi"] = to_u(ps(1, 192), IOFF)
        elif what == "nq":
            gather(w[1], "NP", st["qi"], "R0", int(w[2]), int(w[3]))
        elif what == "wq":
            wrap("R0", NXZ, ps(2), st["nx"])
        elif what == "pp":
            st["p"] = st["c"][1]
            st["pp"] = split(wf(st["p"]))
            form(st["pp"], ps(3, 288), dg(SIXTEENTH), dg(TIMES384))
            st["u"]["c0z"] = to_u(wf(st["p"]), ZOFF)
        elif what == "pu":
            st["u"]["c0i"] = to_u(ps(3, 288), IOFF)
        elif what == "H":
            for n in range(4):
                mm(ps(4 + n, 0, 384), half, blk(zown, blocks[n]), True, False)
                mm(ps(4 + n, 0, 384), quarter, A("CM"), False, False)
        elif what == "ga":
            gather(w[1], "QT", st["pvi"], "R2", int(w[2]), int(w[3]))
        elif what == "wa":
            wrap("R2", NXI, ps(0))
        elif what == "wz":
            wrap("R2", NXZ, ps(3), st["pv"])
        elif what == "ua":
            st["ai"] = to_u(ps(0), IOFF)
        elif what == "gq":
            gather(w[1], "QT", st["qi"], "R1", int(w[2]), int(w[3]))
        elif what == "wqq":
            wrap("R1", NXZ, ps(2, 288))
        elif what == "gb":
            gather(w[1], "QT", st["ai"], "R0", int(w[2]), int(w[3]))
        elif what == "wb":
            wrap("R0", NXZ, ps(0))
        elif what == "NX":
            sw = new("WF")
            tt(wf(sw), ps(2, 288), wf(ident), EQ)
            st["nx"] = pick(wf(st["nx"]), wf(sw), ps(2), ps(2, 192))
            st["nz"] = to_u(wf(st["nx"]), ZOFF)
        elif what == "PVa":
            npc = split(wf(st["nx"]))
            for b in (1, 2):
                mm(ps(b, 0, 192), A("ZB", 0, 128), A("ZB", 0, 192), True, False)
            np_mm(npc, 0, False)
        elif what == "PVb":
            sv = new("WF")
            tt(wf(sv), ps(0), wf(st["pv"]), EQ)
            st["pv"] = pick(wf(st["pv"]), wf(sv), ps(3), ps(3, 192))
            st["vz"] = to_u(wf(st["pv"]), ZOFF)
        elif what == "PVc":
            vpc = split(wf(st["pv"]))
            np_mm(vpc, 1, True)
            form(vpc, ps(3), dg(SIXTEENTH), dg(TIMES384))
            form(st["pp"], CAND[0], dg(PLUS), dg(PLUS))
        elif what == "XN":
            table_out("XN", 128, (1, 2))
            flatten("XN", 128, "NP", 4)
        elif what == "U":
            st["pvi"] = to_u(ps(3), IOFF)
        elif what in "nv":
            n = blocks[int(w[1])]
            gather(w[2], table, st[what + "z"], {"n": "GN", "v": "GP"}[what], 24 * n, 24 * n + 24)
        elif what == "m":
            n = int(w[1])
            mm(ps(4 + n, 0, 384), quarter, blk("GN", blocks[n]), False, False)
            mm(ps(4 + n, 0, 384), quarter, blk("GP", blocks[n]), False, w[2] == "v")
            if w[2] == "a":
                mm(ps(4 + n, 0, 384), quarter, A("CR"), False, True)
            st["round", n] = w[2]
        elif what == "r":
            n = int(w[1])
            if st["round", n] == "v":
                ts(blk(outs[n], blocks[n]), ps(4 + n, 0, 384), M1, M1, ADD, SUB)
            else:
                shift(blk(outs[n], blocks[n]), ps(4 + n, 0, 384), -M1)
            free.insert(0, 4 + n)
        elif what == "LM":
            i, row = {"n": (st["nx"], 0), "v": (st["pv"], 1), "p": (st["c"][1], 2)}[w[1]]
            if w[1] == "p":
                mm(ps(1, 0, 384), A("ZB", 0, 128), A("ZB", 0, 384), True, False)
            for k in range(4):
                o = 192 * k + 64 - 32 * row
                mm(ps(1, 96 * k), A("MH", o, o + 128), wf(i), False, w[1] == "v" and k == 3)
        elif what == "LS":
            for k in range(4):
                shift(X(T.LS[:, :, k, :], "LS", tag=k), ps(1, 96 * k), ZOFF)
        elif w[1] == "l":
            send([(r, X(T.LS[:, r], "LS"), blk("LL", me, 96)[0], "arrm%d" % me) for r in far + near])
        else:
            send([(r, blk("ZS", r), blk("ZL", me)[0], "arrz%d" % me) for r in (far if w[1] == "f" else near)])

    for word in OPT["plan1"].split():
        w = word.split(".")
        if w[0] in "FOfo":
            tables(w, "LAND", [me] + near + far, "ZT", "ZA")
        elif w[0] in ("P", "XL", "L", "Q"):
            begin(w)
        else:
            slide(w, OPT["cuts"][0], "ZT", "ZA")
    for plan, table, zown, blocks, outs in (("plan2", "ZT", "ZA", [0, 1, 2, 3], ["ZP"] * 4),
                                            ("plan3", "ZU", "ZN", far + near + [me], ["ZS", "ZS", "ZS", "ZO"])):
        for word in OPT[plan].split():
            w = word.split(".")
            if w[0] in "FOfo":
                tables(w, "ZP", blocks, "ZU", "ZN")
            elif w[0] in "wuegdbsxthkcq":
                slide(w, OPT["cuts"][1], "ZU", "ZN")
            else:
                swap(w, table, zown, blocks, outs)

    def out_lists(r, q):
        for row, name in enumerate(("yn", "yv", "yp")):
            if r == me:
                src, view = T.LS[32 * row:32 * row + 32, r], A("LS")
            else:
                src, view = T.LL[32 * row:32 * row + 32, 96 * r:96 * r + 96], blk("LL", r, 96)
            stores.append((q, T[name][32 * r:32 * r + 32, :], src, [view], []))

    def out_points(r, q):
        stores.append((q, T.yx[32 * r:32 * r + 32, :], blk("ZO", r)[0], [blk("ZO", r)], []))

    stores = []
    out_lists(me, "s")
    out_points(me, "s")
    out_lists(near[0], "s")
    dmas(stores)
    for r, qn in ((far[0], "a"), (far[1], "v"), (near[0], "v")):
        cp(qn, blk("ZO", r), blk("ZL", r))
    stores = []
    out_points(far[0], "a")
    out_points(far[1], "s")
    out_points(near[0], "s")
    out_lists(far[0], "a")
    out_lists(far[1], "s")
    dmas(stores)
    for s in count:
        wait("g", (s, count[s]))
